import numpy as np
import ml_dtypes


def mxq(x, axis, fmt="e4m3"):
    dtype, down = {"e4m3": (ml_dtypes.float8_e4m3fn, 7), "e5m2": (ml_dtypes.float8_e5m2, 14)}[fmt]
    v = np.moveaxis(np.asarray(x, np.float32).astype(ml_dtypes.bfloat16).astype(np.float64), axis, -1)
    blocks = v.reshape(v.shape[:-1] + (-1, 32))
    amax = np.abs(blocks).max(-1, keepdims=True)
    byte = np.maximum(np.where(amax > 0, np.frexp(amax)[1] - 1 + 127, 0) - down, 1)
    scale = np.exp2(byte - 127.0)
    codes = (blocks / scale).astype(np.float32).astype(dtype).astype(np.float64)
    return np.moveaxis((codes * scale).reshape(v.shape), -1, axis)


WIDE = False


def mx_kscale(k):
    if not WIDE:
        return np.ones(k)
    levels = np.array([10, -10, 5, -5, 0])
    if k % 512:
        return np.exp2(np.random.permutation(np.resize(levels, k // 32))).repeat(32)
    a = np.empty((k // 512, 16))
    for p in range(k // 512):
        a[p, :8] = np.random.permutation(np.resize(levels, 8))
        for g in range(8):
            far = levels[np.abs(levels - a[p, g]) >= 10]
            a[p, g + 8] = far[np.random.randint(len(far))]
    return np.exp2(a.ravel()).repeat(32)


def f64(x):
    return np.asarray(x).astype(np.float64)


E2M1 = np.array([0.0, 0.5, 1.0, 1.5, 2.0, 3.0, 4.0, 6.0, -0.0, -0.5, -1.0, -1.5, -2.0, -3.0, -4.0, -6.0])


def pack_weight(w, fmt):
    k, n = w.shape
    w = f64(np.asarray(w, np.float32).astype(ml_dtypes.bfloat16)).reshape(k // 32, 32, n)
    amax = np.abs(w).max(1)
    if fmt == "e4m3":
        byte = np.frexp(amax)[1] - 1 + 127 - 7
    else:
        mant, ex = np.frexp(amax / 6.0)
        byte = np.where(mant > 0.5, ex, ex - 1) + 127
    byte = np.clip(np.where(amax > 0, byte, 1), 1, 254)
    scaled = (w * np.exp2(127.0 - byte)[:, None, :]).reshape(k, n).astype(np.float32)
    by_word = np.ascontiguousarray(scaled.reshape(k // 512, 128, 4, n).transpose(0, 1, 3, 2))
    if fmt == "e4m3":
        words = by_word.astype(ml_dtypes.float8_e4m3fn).view(np.uint8)
    else:
        c = by_word.astype(ml_dtypes.float4_e2m1fn).view(np.uint8) & 0xF
        words = (c[..., 0::2] | (c[..., 1::2] << 4)).reshape(k // 512, 128, 2 * n)
    return np.ascontiguousarray(words), np.ascontiguousarray(byte.astype(np.uint8).reshape(k // 512, 16, n))


def unpack_weight(words, scales, fmt):
    g, _, n = scales.shape
    words = np.ascontiguousarray(words).reshape(g, 128, n, -1)
    if fmt == "e4m3":
        vals = words.view(ml_dtypes.float8_e4m3fn).astype(np.float64)
    else:
        nib = np.empty((g, 128, n, 4), np.uint8)
        nib[..., 0::2] = words & 0xF
        nib[..., 1::2] = words >> 4
        vals = E2M1[nib]
    vals = vals * np.repeat(np.exp2(scales.astype(np.float64) - 127.0), 8, axis=1)[..., None]
    return vals.transpose(0, 1, 3, 2).reshape(g * 512, n)


K, M, T = 512, 1536, 1024


def setup_inputs():
    n = np.random.standard_normal
    s = mx_kscale(K)[:, None]
    x = n((K, T)) * s
    x4 = pack_weight(x, "e2m1")
    rest = x - unpack_weight(*x4, "e2m1")
    p_w4 = pack_weight(n((K, M)) / np.sqrt(K) / s, "e2m1")
    return {
        "x4_words": x4[0],
        "x4_scales": x4[1],
        "xr": (rest).astype(np.float32),
        "w4_words": p_w4[0],
        "w4_scales": p_w4[1],
        "b": (0.3 * n(1536)).astype(np.float32),
    }


def reference(x4_words, x4_scales, xr, w4_words, w4_scales, b):
    x4_ = unpack_weight(x4_words, x4_scales, "e2m1")
    xr_ = mxq(f64(xr), 0, "e4m3")
    w4_ = unpack_weight(w4_words, w4_scales, "e2m1")
    y = w4_.T @ x4_ + w4_.T @ xr_
    return y + f64(b)[:, None]

@@ -1,0 +1,179 @@
+from contextlib import ExitStack
+
+import concourse.mybir as mybir
+
+F32 = mybir.dt.float32
+BF16 = mybir.dt.bfloat16
+U32 = mybir.dt.uint32
+I32 = mybir.dt.int32
+U8 = mybir.dt.uint8
+FP8X4 = mybir.dt.float8_e4m3fn_x4
+FP4X4 = mybir.dt.float4_e2m1fn_x4
+ADD = mybir.AluOpType.add
+IDENTITY = mybir.ActivationFunctionType.Identity
+
+P = 128
+PACK = 4
+K = P * PACK
+M = 1536
+T = 1024
+HALF = T // 2
+TILES = M // P
+BANKS = 8
+FLOPS = 2 * 2 * K * M * T
+
+SOLO = 7
+LEAD = 5
+
+
+def tile_mix_xres_fm_bias_kernel(tc, x4_words, x4_scales, xr, w4_words, w4_scales, b, out):
+    nc = tc.nc
+    with ExitStack() as ctx:
+        keep = ctx.enter_context(tc.tile_pool(name="keep", bufs=1))
+        outs = ctx.enter_context(tc.tile_pool(name="outs", bufs=TILES))
+        psum = ctx.enter_context(tc.psum_pool(name="psum", bufs=BANKS))
+        ctx.enter_context(tc.manual_schedule())
+
+        zeros = keep.tile([P, 32], F32, name="zeros", align_bytes=256)
+        w4 = keep.tile([P, 2 * M], U8, name="w4", align_bytes=256)
+        w4_plane = keep.tile([P, M], U8, name="w4_plane", align_bytes=256)
+        x4 = keep.tile([P, 2 * T], U8, name="x4", align_bytes=256)
+        x4_plane = keep.tile([P, T], U8, name="x4_plane", align_bytes=256)
+        codes = keep.tile([P, T], U32, name="codes", align_bytes=256)
+        scales = keep.tile([P, T], U8, name="scales", align_bytes=256)
+        raw_lo = keep.tile([P, PACK, HALF], F32, name="raw_lo", align_bytes=256)
+        raw_hi = keep.tile([P, PACK, HALF], F32, name="raw_hi", align_bytes=256)
+        grouped = keep.tile([P, T, PACK], BF16, name="grouped", align_bytes=256)
+        b_rows_lo = keep.tile([P, 32], F32, name="b_rows_lo", align_bytes=256)
+        b_rows_hi = keep.tile([P, 32], F32, name="b_rows_hi", align_bytes=256)
+        b_cols_lo = keep.tile([P, 32], F32, name="b_cols_lo", align_bytes=256)
+        b_cols_hi = keep.tile([P, 32], F32, name="b_cols_hi", align_bytes=256)
+
+        nc.vector.memset(w4_plane[:].bitcast(I32), 0)
+        nc.gpsimd.memset(x4_plane[:].bitcast(I32), 0)
+        nc.vector.memset(zeros[:], 0.0)
+
+        def load_scale_rows(queue, plane, rows, q):
+            queue.dma_start(
+                out=plane[32 * q : 32 * q + 4, :].bitcast(I32),
+                in_=rows[0, 4 * q : 4 * q + 4, :].bitcast(I32),
+            )
+
+        def load_xr(queue, tile, t0, t1):
+            queue.dma_start(out=tile[:], in_=xr[:, t0:t1].rearrange("(p j) t -> p j t", j=PACK))
+
+        load_xr(nc.sync, raw_lo, 0, HALF)
+        nc.sync.dma_start(out=w4[:], in_=w4_words[0])
+        nc.sync.dma_start(out=x4[:], in_=x4_words[0])
+        for q in range(4):
+            load_scale_rows(nc.scalar, w4_plane, w4_scales, q)
+        load_scale_rows(nc.scalar, x4_plane, x4_scales, 0)
+        for q in range(1, 4):
+            load_scale_rows(nc.gpsimd, x4_plane, x4_scales, q)
+        load_xr(nc.gpsimd, raw_hi, HALF, T)
+        nc.scalar.activation(out=b_rows_lo[:], in_=zeros[:], func=IDENTITY)
+        nc.scalar.activation(out=b_rows_hi[:], in_=zeros[:], func=IDENTITY)
+        b_rows = b.rearrange("(k a i) -> a k i", a=4, i=32)
+        nc.sync.dma_start(out=b_rows_lo[0:P:4, :], in_=b_rows[:, 0:8, :])
+        nc.sync.dma_start(out=b_rows_hi[0:P:8, :], in_=b_rows[:, 8:12, :])
+
+        def bias(j):
+            if j < 8:
+                return b_cols_lo[:, 4 * j : 4 * j + 1]
+            return b_cols_hi[:, 8 * (j - 8) : 8 * (j - 8) + 1]
+
+        def cast(copy, tile, origin, t0, t1):
+            copy(out=grouped[:, t0:t1, :], in_=tile[:, :, t0 - origin : t1 - origin].rearrange("p j t -> p t j"))
+
+        def quantize(t0, t1):
+            nc.vector.quantize_mx(
+                out=codes[:, t0:t1].bitcast(FP8X4),
+                scales=scales[:, t0:t1],
+                in_=grouped[:, t0:t1, :].rearrange("p t j -> p (t j)"),
+            )
+
+        def prepare_first_half():
+            cast(nc.vector.tensor_copy, raw_lo, 0, 0, 256)
+            cast(nc.scalar.copy, raw_lo, 0, 320, 512)
+            cast(nc.vector.tensor_copy, raw_lo, 0, 256, 320)
+            quantize(0, 256)
+            quantize(256, 512)
+            nc.vector.transpose(b_cols_lo[:], b_rows_lo[:])
+
+        def prepare_second_half():
+            cast(nc.vector.tensor_copy, raw_hi, HALF, 512, 768)
+            cast(nc.vector.tensor_copy, raw_hi, HALF, 768, 1024)
+            quantize(512, 768)
+            quantize(768, 1024)
+            nc.vector.transpose(b_cols_hi[:], b_rows_hi[:])
+
+        units = [(j, 0) for j in range(SOLO)]
+        units += [(j, h) for j in range(SOLO, TILES) for h in range(2)]
+        units += [(j, 1) for j in range(SOLO)]
+        accs = {}
+        results = {}
+
+        def add_product(u, rhs, rhs_scale, start, stop):
+            j = units[u][0]
+            nc.tensor.matmul_mx(
+                out=accs[u][:],
+                lhsT=w4[:, 2 * P * j : 2 * P * (j + 1)].bitcast(FP4X4),
+                lhsT_scale=w4_plane[:, P * j : P * (j + 1)],
+                rhs=rhs,
+                rhs_scale=rhs_scale,
+                start=start,
+                stop=stop,
+            )
+
+        def add_x4(u, start):
+            h = units[u][1]
+            words = slice(2 * HALF * h, 2 * HALF * (h + 1))
+            cols = slice(HALF * h, HALF * (h + 1))
+            add_product(u, x4[:, words].bitcast(FP4X4), x4_plane[:, cols], start, not start)
+
+        def add_xr(u, start):
+            h = units[u][1]
+            cols = slice(HALF * h, HALF * (h + 1))
+            add_product(u, codes[:, cols].bitcast(FP8X4), scales[:, cols], start, not start)
+
+        def open_unit(u):
+            acc = psum.tile([P, HALF], F32, name="acc")
+            accs[u] = acc
+            if units[u][1] == 0:
+                add_xr(u, True)
+            else:
+                add_x4(u, True)
+
+        def close_unit(u):
+            if units[u][1] == 0:
+                add_x4(u, False)
+            else:
+                add_xr(u, False)
+
+        def drain_unit(u):
+            j, h = units[u]
+            if j not in results:
+                o = outs.tile([P, T], F32, name="o", align_bytes=256)
+                results[j] = o
+            o = results[j]
+            cols = slice(HALF * h, HALF * (h + 1))
+            if u in (0, 2, 7) or (u >= 8 and u % 2 == 0):
+                nc.vector.tensor_scalar(out=o[:, cols], in0=accs[u][:], scalar1=bias(j), scalar2=None, op0=ADD)
+            else:
+                nc.scalar.activation(out=o[:, cols], in_=accs[u][:], func=IDENTITY, bias=bias(j))
+            rows = slice(P * j, P * (j + 1))
+            if j < SOLO:
+                nc.sync.dma_start(out=out[rows, cols], in_=o[:, cols])
+            elif h == 1:
+                nc.sync.dma_start(out=out[rows, :], in_=o[:])
+
+        prepare_first_half()
+        opened = 0
+        for u in range(len(units)):
+            while opened < min(len(units), u + 1 + min(LEAD, u // 2)):
+                open_unit(opened)
+                opened += 1
+            if u == 4:
+                prepare_second_half()
+            close_unit(u)
+            drain_unit(u)

@@ -18,12 +18,14 @@ K = P * PACK
 M = 1536
 T = 1024
 HALF = T // 2
+QUARTER = T // 4
 TILES = M // P
 BANKS = 8
 FLOPS = 2 * 2 * K * M * T
 
 SOLO = 7
-LEAD = 5
+EARLY = 8
+LEAD = 2
 
 
 def tile_mix_xres_fm_bias_kernel(tc, x4_words, x4_scales, xr, w4_words, w4_scales, b, out):
@@ -34,53 +36,48 @@ def tile_mix_xres_fm_bias_kernel(tc, x4_words, x4_scales, xr, w4_words, w4_scale
         psum = ctx.enter_context(tc.psum_pool(name="psum", bufs=BANKS))
         ctx.enter_context(tc.manual_schedule())
 
-        zeros = keep.tile([P, 32], F32, name="zeros", align_bytes=256)
         w4 = keep.tile([P, 2 * M], U8, name="w4", align_bytes=256)
         w4_plane = keep.tile([P, M], U8, name="w4_plane", align_bytes=256)
         x4 = keep.tile([P, 2 * T], U8, name="x4", align_bytes=256)
         x4_plane = keep.tile([P, T], U8, name="x4_plane", align_bytes=256)
         codes = keep.tile([P, T], U32, name="codes", align_bytes=256)
         scales = keep.tile([P, T], U8, name="scales", align_bytes=256)
-        raw_lo = keep.tile([P, PACK, HALF], F32, name="raw_lo", align_bytes=256)
+        raw_a = keep.tile([P, PACK, QUARTER], F32, name="raw_a", align_bytes=256)
+        raw_b = keep.tile([P, PACK, QUARTER], F32, name="raw_b", align_bytes=256)
         raw_hi = keep.tile([P, PACK, HALF], F32, name="raw_hi", align_bytes=256)
         grouped = keep.tile([P, T, PACK], BF16, name="grouped", align_bytes=256)
-        b_rows_lo = keep.tile([P, 32], F32, name="b_rows_lo", align_bytes=256)
-        b_rows_hi = keep.tile([P, 32], F32, name="b_rows_hi", align_bytes=256)
-        b_cols_lo = keep.tile([P, 32], F32, name="b_cols_lo", align_bytes=256)
-        b_cols_hi = keep.tile([P, 32], F32, name="b_cols_hi", align_bytes=256)
+        b_rows = keep.tile([P, TILES * 32], F32, name="b_rows", align_bytes=256)
+        b_cols = keep.tile([P, TILES * 32], F32, name="b_cols", align_bytes=256)
+        warm = keep.tile([P, 16], F32, name="warm", align_bytes=256)
 
-        nc.vector.memset(w4_plane[:].bitcast(I32), 0)
+        nc.gpsimd.memset(w4_plane[:].bitcast(I32), 0)
         nc.gpsimd.memset(x4_plane[:].bitcast(I32), 0)
-        nc.vector.memset(zeros[:], 0.0)
+        nc.vector.memset(warm[:, 0:1], 0.0)
+        nc.vector.memset(b_rows[:], 0.0)
 
-        def load_scale_rows(queue, plane, rows, q):
-            queue.dma_start(
-                out=plane[32 * q : 32 * q + 4, :].bitcast(I32),
-                in_=rows[0, 4 * q : 4 * q + 4, :].bitcast(I32),
-            )
+        def load_scale_rows(queue, plane, rows, r):
+            queue.dma_start(out=plane[r:P:32, :].bitcast(I32), in_=rows[0, r:16:4, :].bitcast(I32))
 
         def load_xr(queue, tile, t0, t1):
             queue.dma_start(out=tile[:], in_=xr[:, t0:t1].rearrange("(p j) t -> p j t", j=PACK))
 
-        load_xr(nc.sync, raw_lo, 0, HALF)
+        load_xr(nc.sync, raw_a, 0, QUARTER)
+        for r in range(4):
+            load_scale_rows(nc.sync, w4_plane, w4_scales, r)
         nc.sync.dma_start(out=w4[:], in_=w4_words[0])
+        load_xr(nc.sync, raw_b, QUARTER, HALF)
+        for r in range(4):
+            load_scale_rows(nc.sync, x4_plane, x4_scales, r)
+        nc.sync.dma_start(
+            out=b_rows[0:P:32, :].rearrange("a (j i) -> a j i", i=32),
+            in_=b.rearrange("(j a i) -> a j i", a=4, i=32),
+        )
         nc.sync.dma_start(out=x4[:], in_=x4_words[0])
-        for q in range(4):
-            load_scale_rows(nc.scalar, w4_plane, w4_scales, q)
-        load_scale_rows(nc.scalar, x4_plane, x4_scales, 0)
-        for q in range(1, 4):
-            load_scale_rows(nc.gpsimd, x4_plane, x4_scales, q)
-        load_xr(nc.gpsimd, raw_hi, HALF, T)
-        nc.scalar.activation(out=b_rows_lo[:], in_=zeros[:], func=IDENTITY)
-        nc.scalar.activation(out=b_rows_hi[:], in_=zeros[:], func=IDENTITY)
-        b_rows = b.rearrange("(k a i) -> a k i", a=4, i=32)
-        nc.sync.dma_start(out=b_rows_lo[0:P:4, :], in_=b_rows[:, 0:8, :])
-        nc.sync.dma_start(out=b_rows_hi[0:P:8, :], in_=b_rows[:, 8:12, :])
+        load_xr(nc.sync, raw_hi, HALF, T)
+        nc.scalar.activation(out=warm[:, 8:9], in_=warm[:, 0:1], func=IDENTITY)
 
         def bias(j):
-            if j < 8:
-                return b_cols_lo[:, 4 * j : 4 * j + 1]
-            return b_cols_hi[:, 8 * (j - 8) : 8 * (j - 8) + 1]
+            return b_cols[:, 32 * j : 32 * j + 1]
 
         def cast(copy, tile, origin, t0, t1):
             copy(out=grouped[:, t0:t1, :], in_=tile[:, :, t0 - origin : t1 - origin].rearrange("p j t -> p t j"))
@@ -92,20 +89,16 @@ def tile_mix_xres_fm_bias_kernel(tc, x4_words, x4_scales, xr, w4_words, w4_scale
                 in_=grouped[:, t0:t1, :].rearrange("p t j -> p (t j)"),
             )
 
-        def prepare_first_half():
-            cast(nc.vector.tensor_copy, raw_lo, 0, 0, 256)
-            cast(nc.scalar.copy, raw_lo, 0, 320, 512)
-            cast(nc.vector.tensor_copy, raw_lo, 0, 256, 320)
-            quantize(0, 256)
-            quantize(256, 512)
-            nc.vector.transpose(b_cols_lo[:], b_rows_lo[:])
+        def prepare_quarter(tile, origin):
+            cast(nc.vector.tensor_copy, tile, origin, origin, origin + 160)
+            cast(nc.scalar.copy, tile, origin, origin + 160, origin + QUARTER)
+            quantize(origin, origin + QUARTER)
 
         def prepare_second_half():
             cast(nc.vector.tensor_copy, raw_hi, HALF, 512, 768)
             cast(nc.vector.tensor_copy, raw_hi, HALF, 768, 1024)
             quantize(512, 768)
             quantize(768, 1024)
-            nc.vector.transpose(b_cols_hi[:], b_rows_hi[:])
 
         units = [(j, 0) for j in range(SOLO)]
         units += [(j, h) for j in range(SOLO, TILES) for h in range(2)]
@@ -113,10 +106,10 @@ def tile_mix_xres_fm_bias_kernel(tc, x4_words, x4_scales, xr, w4_words, w4_scale
         accs = {}
         results = {}
 
-        def add_product(u, rhs, rhs_scale, start, stop):
+        def add_product(u, lo, hi, rhs, rhs_scale, start, stop):
             j = units[u][0]
             nc.tensor.matmul_mx(
-                out=accs[u][:],
+                out=accs[u][:, lo:hi],
                 lhsT=w4[:, 2 * P * j : 2 * P * (j + 1)].bitcast(FP4X4),
                 lhsT_scale=w4_plane[:, P * j : P * (j + 1)],
                 rhs=rhs,
@@ -125,30 +118,34 @@ def tile_mix_xres_fm_bias_kernel(tc, x4_words, x4_scales, xr, w4_words, w4_scale
                 stop=stop,
             )
 
-        def add_x4(u, start):
-            h = units[u][1]
-            words = slice(2 * HALF * h, 2 * HALF * (h + 1))
-            cols = slice(HALF * h, HALF * (h + 1))
-            add_product(u, x4[:, words].bitcast(FP4X4), x4_plane[:, cols], start, not start)
+        def add_x4(u, lo, hi, start, stop):
+            t0 = HALF * units[u][1]
+            words = slice(2 * (t0 + lo), 2 * (t0 + hi))
+            add_product(u, lo, hi, x4[:, words].bitcast(FP4X4), x4_plane[:, t0 + lo : t0 + hi], start, stop)
 
-        def add_xr(u, start):
-            h = units[u][1]
-            cols = slice(HALF * h, HALF * (h + 1))
-            add_product(u, codes[:, cols].bitcast(FP8X4), scales[:, cols], start, not start)
+        def add_xr(u, lo, hi, start, stop):
+            t0 = HALF * units[u][1]
+            cols = slice(t0 + lo, t0 + hi)
+            add_product(u, lo, hi, codes[:, cols].bitcast(FP8X4), scales[:, cols], start, stop)
 
-        def open_unit(u):
+        def new_bank(u):
             acc = psum.tile([P, HALF], F32, name="acc")
             accs[u] = acc
-            if units[u][1] == 0:
-                add_xr(u, True)
+
+        def open_unit(u):
+            if u < EARLY:
+                add_x4(u, 0, QUARTER, False, False)
+                add_x4(u, QUARTER, HALF, False, False)
             else:
-                add_x4(u, True)
+                new_bank(u)
+                add_x4(u, 0, HALF, True, False)
 
         def close_unit(u):
-            if units[u][1] == 0:
-                add_x4(u, False)
+            if u < EARLY:
+                add_xr(u, QUARTER, QUARTER + P, False, False)
+                add_xr(u, QUARTER + P, HALF, False, True)
             else:
-                add_xr(u, False)
+                add_xr(u, 0, HALF, False, True)
 
         def drain_unit(u):
             j, h = units[u]
@@ -157,7 +154,7 @@ def tile_mix_xres_fm_bias_kernel(tc, x4_words, x4_scales, xr, w4_words, w4_scale
                 results[j] = o
             o = results[j]
             cols = slice(HALF * h, HALF * (h + 1))
-            if u in (0, 2, 7) or (u >= 8 and u % 2 == 0):
+            if u in (0, 2) or (u >= 8 and u % 2 == 0):
                 nc.vector.tensor_scalar(out=o[:, cols], in0=accs[u][:], scalar1=bias(j), scalar2=None, op0=ADD)
             else:
                 nc.scalar.activation(out=o[:, cols], in_=accs[u][:], func=IDENTITY, bias=bias(j))
@@ -167,13 +164,20 @@ def tile_mix_xres_fm_bias_kernel(tc, x4_words, x4_scales, xr, w4_words, w4_scale
             elif h == 1:
                 nc.sync.dma_start(out=out[rows, :], in_=o[:])
 
-        prepare_first_half()
+        prepare_quarter(raw_a, 0)
+        for u in range(EARLY):
+            new_bank(u)
+            add_xr(u, 0, P, True, False)
+            add_xr(u, P, QUARTER, False, False)
+        prepare_quarter(raw_b, QUARTER)
+        nc.vector.transpose(b_cols[:, 0:128], b_rows[:, 0:128])
         opened = 0
         for u in range(len(units)):
-            while opened < min(len(units), u + 1 + min(LEAD, u // 2)):
+            while opened < min(len(units), u + 1 + LEAD):
                 open_unit(opened)
                 opened += 1
-            if u == 4:
+            if u == 3:
+                nc.vector.transpose(b_cols[:, 128:384], b_rows[:, 128:384])
                 prepare_second_half()
             close_unit(u)
             drain_unit(u)

@@ -25,14 +25,14 @@ FLOPS = 2 * 2 * K * M * T
 
 SOLO = 7
 EARLY = 8
-LEAD = 2
+AHEAD = 3
+LEAD = 1
 
 
 def tile_mix_xres_fm_bias_kernel(tc, x4_words, x4_scales, xr, w4_words, w4_scales, b, out):
     nc = tc.nc
     with ExitStack() as ctx:
         keep = ctx.enter_context(tc.tile_pool(name="keep", bufs=1))
-        outs = ctx.enter_context(tc.tile_pool(name="outs", bufs=TILES))
         psum = ctx.enter_context(tc.psum_pool(name="psum", bufs=BANKS))
         ctx.enter_context(tc.manual_schedule())
 
@@ -48,6 +48,7 @@ def tile_mix_xres_fm_bias_kernel(tc, x4_words, x4_scales, xr, w4_words, w4_scale
         grouped = keep.tile([P, T, PACK], BF16, name="grouped", align_bytes=256)
         b_rows = keep.tile([P, TILES * 32], F32, name="b_rows", align_bytes=256)
         b_cols = keep.tile([P, TILES * 32], F32, name="b_cols", align_bytes=256)
+        result = keep.tile([P, TILES, T], F32, name="result", align_bytes=256)
         warm = keep.tile([P, 16], F32, name="warm", align_bytes=256)
 
         nc.gpsimd.memset(w4_plane[:].bitcast(I32), 0)
@@ -76,9 +77,6 @@ def tile_mix_xres_fm_bias_kernel(tc, x4_words, x4_scales, xr, w4_words, w4_scale
         load_xr(nc.sync, raw_hi, HALF, T)
         nc.scalar.activation(out=warm[:, 8:9], in_=warm[:, 0:1], func=IDENTITY)
 
-        def bias(j):
-            return b_cols[:, 32 * j : 32 * j + 1]
-
         def cast(copy, tile, origin, t0, t1):
             copy(out=grouped[:, t0:t1, :], in_=tile[:, :, t0 - origin : t1 - origin].rearrange("p j t -> p t j"))
 
@@ -100,16 +98,16 @@ def tile_mix_xres_fm_bias_kernel(tc, x4_words, x4_scales, xr, w4_words, w4_scale
             quantize(512, 768)
             quantize(768, 1024)
 
-        units = [(j, 0) for j in range(SOLO)]
-        units += [(j, h) for j in range(SOLO, TILES) for h in range(2)]
-        units += [(j, 1) for j in range(SOLO)]
-        accs = {}
-        results = {}
+        banks = {}
 
-        def add_product(u, lo, hi, rhs, rhs_scale, start, stop):
-            j = units[u][0]
+        def add_product(unit, t0, t1, rhs, rhs_scale, stop):
+            j, origin = unit
+            start = unit not in banks
+            if start:
+                acc = psum.tile([P, HALF], F32, name="acc")
+                banks[unit] = acc
             nc.tensor.matmul_mx(
-                out=accs[u][:, lo:hi],
+                out=banks[unit][:, t0 - origin : t1 - origin],
                 lhsT=w4[:, 2 * P * j : 2 * P * (j + 1)].bitcast(FP4X4),
                 lhsT_scale=w4_plane[:, P * j : P * (j + 1)],
                 rhs=rhs,
@@ -118,66 +116,62 @@ def tile_mix_xres_fm_bias_kernel(tc, x4_words, x4_scales, xr, w4_words, w4_scale
                 stop=stop,
             )
 
-        def add_x4(u, lo, hi, start, stop):
-            t0 = HALF * units[u][1]
-            words = slice(2 * (t0 + lo), 2 * (t0 + hi))
-            add_product(u, lo, hi, x4[:, words].bitcast(FP4X4), x4_plane[:, t0 + lo : t0 + hi], start, stop)
+        def add_x4(unit, t0, t1, stop=False):
+            add_product(unit, t0, t1, x4[:, 2 * t0 : 2 * t1].bitcast(FP4X4), x4_plane[:, t0:t1], stop)
 
-        def add_xr(u, lo, hi, start, stop):
-            t0 = HALF * units[u][1]
-            cols = slice(t0 + lo, t0 + hi)
-            add_product(u, lo, hi, codes[:, cols].bitcast(FP8X4), scales[:, cols], start, stop)
+        def add_xr(unit, t0, t1, stop=False):
+            step = HALF if t1 - t0 == HALF else P
+            for t in range(t0, t1, step):
+                last = stop and t + step == t1
+                add_product(unit, t, t + step, codes[:, t : t + step].bitcast(FP8X4), scales[:, t : t + step], last)
 
-        def new_bank(u):
-            acc = psum.tile([P, HALF], F32, name="acc")
-            accs[u] = acc
-
-        def open_unit(u):
-            if u < EARLY:
-                add_x4(u, 0, QUARTER, False, False)
-                add_x4(u, QUARTER, HALF, False, False)
+        def drain(unit, on_vector):
+            j, t0 = unit
+            o = result[:, j, t0 : t0 + HALF]
+            bias = b_cols[:, 32 * j : 32 * j + 1]
+            if on_vector:
+                nc.vector.tensor_scalar(out=o, in0=banks[unit][:], scalar1=bias, scalar2=None, op0=ADD)
             else:
-                new_bank(u)
-                add_x4(u, 0, HALF, True, False)
+                nc.scalar.activation(out=o, in_=banks[unit][:], func=IDENTITY, bias=bias)
 
-        def close_unit(u):
-            if u < EARLY:
-                add_xr(u, QUARTER, QUARTER + P, False, False)
-                add_xr(u, QUARTER + P, HALF, False, True)
-            else:
-                add_xr(u, 0, HALF, False, True)
+        out_tiles = out.rearrange("(j p) t -> p j t", p=P)
 
-        def drain_unit(u):
-            j, h = units[u]
-            if j not in results:
-                o = outs.tile([P, T], F32, name="o", align_bytes=256)
-                results[j] = o
-            o = results[j]
-            cols = slice(HALF * h, HALF * (h + 1))
-            if u in (0, 2) or (u >= 8 and u % 2 == 0):
-                nc.vector.tensor_scalar(out=o[:, cols], in0=accs[u][:], scalar1=bias(j), scalar2=None, op0=ADD)
-            else:
-                nc.scalar.activation(out=o[:, cols], in_=accs[u][:], func=IDENTITY, bias=bias(j))
-            rows = slice(P * j, P * (j + 1))
-            if j < SOLO:
-                nc.sync.dma_start(out=out[rows, cols], in_=o[:, cols])
-            elif h == 1:
-                nc.sync.dma_start(out=out[rows, :], in_=o[:])
+        def store(j0, j1, t0, t1):
+            nc.sync.dma_start(out=out_tiles[:, j0:j1, t0:t1], in_=result[:, j0:j1, t0:t1])
+
+        first_stores = {0: 0, 1: 1, 3: 2, 5: 4, 6: 6}
+        whole_stores = {7: 7, 9: 8, 11: 10}
+        last_stores = {2: 0, 5: 3, 6: 6}
 
         prepare_quarter(raw_a, 0)
-        for u in range(EARLY):
-            new_bank(u)
-            add_xr(u, 0, P, True, False)
-            add_xr(u, P, QUARTER, False, False)
+        for j in range(EARLY):
+            add_xr((j, 0), 0, QUARTER)
         prepare_quarter(raw_b, QUARTER)
         nc.vector.transpose(b_cols[:, 0:128], b_rows[:, 0:128])
-        opened = 0
-        for u in range(len(units)):
-            while opened < min(len(units), u + 1 + LEAD):
-                open_unit(opened)
-                opened += 1
-            if u == 3:
+        for j in range(SOLO + AHEAD):
+            if j < EARLY:
+                add_x4((j, 0), 0, QUARTER)
+                add_x4((j, 0), QUARTER, HALF)
+                add_xr((j, 0), QUARTER, HALF, stop=True)
+            else:
+                add_x4((j, 0), 0, HALF)
+                add_xr((j, 0), 0, HALF, stop=True)
+            if j == 3:
                 nc.vector.transpose(b_cols[:, 128:384], b_rows[:, 128:384])
                 prepare_second_half()
-            close_unit(u)
-            drain_unit(u)
+            drain((j, 0), j in (0, 2, SOLO + AHEAD - 1))
+            if j in first_stores:
+                store(first_stores[j], j + 1, 0, HALF)
+        units = [(j, HALF) for j in range(SOLO, SOLO + AHEAD)]
+        units += [(j, t0) for j in range(SOLO + AHEAD, TILES) for t0 in (0, HALF)]
+        units += [(j, HALF) for j in range(SOLO)]
+        for u, (j, t0) in enumerate(units):
+            for ahead in units[: u + 1 + LEAD]:
+                if ahead not in banks:
+                    add_x4(ahead, ahead[1], ahead[1] + HALF)
+            add_xr((j, t0), t0, t0 + HALF, stop=True)
+            drain((j, t0), u % 2 == 1)
+            if t0 == HALF and j in whole_stores:
+                store(whole_stores[j], j + 1, 0, T)
+            if t0 == HALF and j in last_stores:
+                store(last_stores[j], j + 1, HALF, T)

@@ -23,10 +23,10 @@ TILES = M // P
 BANKS = 8
 FLOPS = 2 * 2 * K * M * T
 
-SOLO = 7
-EARLY = 8
-AHEAD = 3
-LEAD = 1
+SOLO = 9
+EARLY = 7
+AHEAD = 0
+LEAD = 0
 
 
 def tile_mix_xres_fm_bias_kernel(tc, x4_words, x4_scales, xr, w4_words, w4_scales, b, out):
@@ -65,7 +65,7 @@ def tile_mix_xres_fm_bias_kernel(tc, x4_words, x4_scales, xr, w4_words, w4_scale
         load_xr(nc.sync, raw_a, 0, QUARTER)
         for r in range(4):
             load_scale_rows(nc.sync, w4_plane, w4_scales, r)
-        nc.sync.dma_start(out=w4[:], in_=w4_words[0])
+        nc.sync.dma_start(out=w4[:, :2048], in_=w4_words[0, :, :2048])
         load_xr(nc.sync, raw_b, QUARTER, HALF)
         for r in range(4):
             load_scale_rows(nc.sync, x4_plane, x4_scales, r)
@@ -73,8 +73,10 @@ def tile_mix_xres_fm_bias_kernel(tc, x4_words, x4_scales, xr, w4_words, w4_scale
             out=b_rows[0:P:32, :].rearrange("a (j i) -> a j i", i=32),
             in_=b.rearrange("(j a i) -> a j i", a=4, i=32),
         )
-        nc.sync.dma_start(out=x4[:], in_=x4_words[0])
+        nc.sync.dma_start(out=x4[:, :T], in_=x4_words[0, :, :T])
         load_xr(nc.sync, raw_hi, HALF, T)
+        nc.sync.dma_start(out=w4[:, 2048:], in_=w4_words[0, :, 2048:])
+        nc.sync.dma_start(out=x4[:, T:], in_=x4_words[0, :, T:])
         nc.scalar.activation(out=warm[:, 8:9], in_=warm[:, 0:1], func=IDENTITY)
 
         def cast(copy, tile, origin, t0, t1):
@@ -139,15 +141,16 @@ def tile_mix_xres_fm_bias_kernel(tc, x4_words, x4_scales, xr, w4_words, w4_scale
         def store(j0, j1, t0, t1):
             nc.sync.dma_start(out=out_tiles[:, j0:j1, t0:t1], in_=result[:, j0:j1, t0:t1])
 
-        first_stores = {0: 0, 1: 1, 3: 2, 5: 4, 6: 6}
-        whole_stores = {7: 7, 9: 8, 11: 10}
-        last_stores = {2: 0, 5: 3, 6: 6}
+        first_stores = {0: 0, 1: 1, 2: 2, 4: 3, 6: 5, 8: 7}
+        whole_stores = {9: 9, 10: 10, 11: 11}
+        last_stores = {1: 0, 3: 2, 5: 4, 7: 6, 8: 8}
 
         prepare_quarter(raw_a, 0)
         for j in range(EARLY):
             add_xr((j, 0), 0, QUARTER)
         prepare_quarter(raw_b, QUARTER)
         nc.vector.transpose(b_cols[:, 0:128], b_rows[:, 0:128])
+        nc.vector.transpose(b_cols[:, 128:384], b_rows[:, 128:384])
         for j in range(SOLO + AHEAD):
             if j < EARLY:
                 add_x4((j, 0), 0, QUARTER)
@@ -157,9 +160,8 @@ def tile_mix_xres_fm_bias_kernel(tc, x4_words, x4_scales, xr, w4_words, w4_scale
                 add_x4((j, 0), 0, HALF)
                 add_xr((j, 0), 0, HALF, stop=True)
             if j == 3:
-                nc.vector.transpose(b_cols[:, 128:384], b_rows[:, 128:384])
                 prepare_second_half()
-            drain((j, 0), j in (0, 2, SOLO + AHEAD - 1))
+            drain((j, 0), j in (0, 2, SOLO - 1))
             if j in first_stores:
                 store(first_stores[j], j + 1, 0, HALF)
         units = [(j, HALF) for j in range(SOLO, SOLO + AHEAD)]

@@ -23,9 +23,9 @@ TILES = M // P
 BANKS = 8
 FLOPS = 2 * 2 * K * M * T
 
-SOLO = 9
+SOLO = 7
 EARLY = 7
-AHEAD = 0
+AHEAD = 2
 LEAD = 0
 
 
@@ -51,8 +51,8 @@ def tile_mix_xres_fm_bias_kernel(tc, x4_words, x4_scales, xr, w4_words, w4_scale
         result = keep.tile([P, TILES, T], F32, name="result", align_bytes=256)
         warm = keep.tile([P, 16], F32, name="warm", align_bytes=256)
 
-        nc.gpsimd.memset(w4_plane[:].bitcast(I32), 0)
         nc.gpsimd.memset(x4_plane[:].bitcast(I32), 0)
+        nc.vector.memset(w4_plane[:].bitcast(I32), 0)
         nc.vector.memset(warm[:, 0:1], 0.0)
         nc.vector.memset(b_rows[:], 0.0)
 
@@ -63,11 +63,13 @@ def tile_mix_xres_fm_bias_kernel(tc, x4_words, x4_scales, xr, w4_words, w4_scale
             queue.dma_start(out=tile[:], in_=xr[:, t0:t1].rearrange("(p j) t -> p j t", j=PACK))
 
         load_xr(nc.sync, raw_a, 0, QUARTER)
+        for r in range(2):
+            load_scale_rows(nc.gpsimd, x4_plane, x4_scales, r)
         for r in range(4):
             load_scale_rows(nc.sync, w4_plane, w4_scales, r)
         nc.sync.dma_start(out=w4[:, :2048], in_=w4_words[0, :, :2048])
         load_xr(nc.sync, raw_b, QUARTER, HALF)
-        for r in range(4):
+        for r in range(2, 4):
             load_scale_rows(nc.sync, x4_plane, x4_scales, r)
         nc.sync.dma_start(
             out=b_rows[0:P:32, :].rearrange("a (j i) -> a j i", i=32),
@@ -141,9 +143,9 @@ def tile_mix_xres_fm_bias_kernel(tc, x4_words, x4_scales, xr, w4_words, w4_scale
         def store(j0, j1, t0, t1):
             nc.sync.dma_start(out=out_tiles[:, j0:j1, t0:t1], in_=result[:, j0:j1, t0:t1])
 
-        first_stores = {0: 0, 1: 1, 2: 2, 4: 3, 6: 5, 8: 7}
-        whole_stores = {9: 9, 10: 10, 11: 11}
-        last_stores = {1: 0, 3: 2, 5: 4, 7: 6, 8: 8}
+        first_stores = {0: 0, 1: 1, 2: 2, 4: 3, 6: 5}
+        whole_stores = {7: 7, 8: 8, 9: 9, 10: 10, 11: 11}
+        last_stores = {2: 0, 5: 3, 6: 6}
 
         prepare_quarter(raw_a, 0)
         for j in range(EARLY):
@@ -161,7 +163,7 @@ def tile_mix_xres_fm_bias_kernel(tc, x4_words, x4_scales, xr, w4_words, w4_scale
                 add_xr((j, 0), 0, HALF, stop=True)
             if j == 3:
                 prepare_second_half()
-            drain((j, 0), j in (0, 2, SOLO - 1))
+            drain((j, 0), j in (0, 2, SOLO + AHEAD - 1))
             if j in first_stores:
                 store(first_stores[j], j + 1, 0, HALF)
         units = [(j, HALF) for j in range(SOLO, SOLO + AHEAD)]

@@ -21,12 +21,14 @@ HALF = T // 2
 QUARTER = T // 4
 TILES = M // P
 BANKS = 8
+QUADRANT = 32
 FLOPS = 2 * 2 * K * M * T
 
-SOLO = 7
-EARLY = 7
-AHEAD = 2
-LEAD = 0
+QUARTER_TILES = 3
+HALF_TILES = 6
+EARLY_TILES = 4
+VECTOR_SHARE = 160
+W4_FIRST_TILES = 8
 
 
 def tile_mix_xres_fm_bias_kernel(tc, x4_words, x4_scales, xr, w4_words, w4_scales, b, out):
@@ -37,74 +39,76 @@ def tile_mix_xres_fm_bias_kernel(tc, x4_words, x4_scales, xr, w4_words, w4_scale
         ctx.enter_context(tc.manual_schedule())
 
         w4 = keep.tile([P, 2 * M], U8, name="w4", align_bytes=256)
-        w4_plane = keep.tile([P, M], U8, name="w4_plane", align_bytes=256)
+        w4_scale = keep.tile([P, M], U8, name="w4_scale", align_bytes=256)
         x4 = keep.tile([P, 2 * T], U8, name="x4", align_bytes=256)
-        x4_plane = keep.tile([P, T], U8, name="x4_plane", align_bytes=256)
-        codes = keep.tile([P, T], U32, name="codes", align_bytes=256)
-        scales = keep.tile([P, T], U8, name="scales", align_bytes=256)
-        raw_a = keep.tile([P, PACK, QUARTER], F32, name="raw_a", align_bytes=256)
-        raw_b = keep.tile([P, PACK, QUARTER], F32, name="raw_b", align_bytes=256)
+        x4_scale = keep.tile([P, T], U8, name="x4_scale", align_bytes=256)
+        xr_codes = keep.tile([P, T], U32, name="xr_codes", align_bytes=256)
+        xr_scale = keep.tile([P, T], U8, name="xr_scale", align_bytes=256)
+        raw_q0 = keep.tile([P, PACK, QUARTER], F32, name="raw_q0", align_bytes=256)
+        raw_q1 = keep.tile([P, PACK, QUARTER], F32, name="raw_q1", align_bytes=256)
         raw_hi = keep.tile([P, PACK, HALF], F32, name="raw_hi", align_bytes=256)
         grouped = keep.tile([P, T, PACK], BF16, name="grouped", align_bytes=256)
-        b_rows = keep.tile([P, TILES * 32], F32, name="b_rows", align_bytes=256)
-        b_cols = keep.tile([P, TILES * 32], F32, name="b_cols", align_bytes=256)
+        b_rows = keep.tile([P, TILES * QUADRANT], F32, name="b_rows", align_bytes=256)
+        b_cols = keep.tile([P, TILES * QUADRANT], F32, name="b_cols", align_bytes=256)
         result = keep.tile([P, TILES, T], F32, name="result", align_bytes=256)
-        warm = keep.tile([P, 16], F32, name="warm", align_bytes=256)
+        zero = keep.tile([P, 1], F32, name="zero", align_bytes=256)
 
-        nc.gpsimd.memset(x4_plane[:].bitcast(I32), 0)
-        nc.vector.memset(w4_plane[:].bitcast(I32), 0)
-        nc.vector.memset(warm[:, 0:1], 0.0)
-        nc.vector.memset(b_rows[:], 0.0)
+        nc.gpsimd.memset(x4_scale[:].bitcast(I32), 0)
+        nc.vector.memset(zero[:], 0.0)
+        nc.vector.memset(w4_scale[:].bitcast(I32), 0)
+        nc.scalar.activation(out=b_rows[:], in_=zero[:].to_broadcast([P, TILES * QUADRANT]), func=IDENTITY)
 
-        def load_scale_rows(queue, plane, rows, r):
-            queue.dma_start(out=plane[r:P:32, :].bitcast(I32), in_=rows[0, r:16:4, :].bitcast(I32))
+        def load_scale_rows(queue, scale, rows, r):
+            queue.dma_start(out=scale[r:P:QUADRANT, :].bitcast(I32), in_=rows[0, r:16:4, :].bitcast(I32))
 
-        def load_xr(queue, tile, t0, t1):
-            queue.dma_start(out=tile[:], in_=xr[:, t0:t1].rearrange("(p j) t -> p j t", j=PACK))
+        def load_xr(raw, t0, t1):
+            nc.sync.dma_start(out=raw[:], in_=xr[:, t0:t1].rearrange("(p i) t -> p i t", i=PACK))
 
-        load_xr(nc.sync, raw_a, 0, QUARTER)
+        w4_cut = 2 * P * W4_FIRST_TILES
+        load_xr(raw_q0, 0, QUARTER)
         for r in range(2):
-            load_scale_rows(nc.gpsimd, x4_plane, x4_scales, r)
+            load_scale_rows(nc.gpsimd, x4_scale, x4_scales, r)
         for r in range(4):
-            load_scale_rows(nc.sync, w4_plane, w4_scales, r)
-        nc.sync.dma_start(out=w4[:, :2048], in_=w4_words[0, :, :2048])
-        load_xr(nc.sync, raw_b, QUARTER, HALF)
+            load_scale_rows(nc.sync, w4_scale, w4_scales, r)
+        nc.sync.dma_start(out=w4[:, :w4_cut], in_=w4_words[0, :, :w4_cut])
+        load_xr(raw_q1, QUARTER, HALF)
         for r in range(2, 4):
-            load_scale_rows(nc.sync, x4_plane, x4_scales, r)
+            load_scale_rows(nc.sync, x4_scale, x4_scales, r)
         nc.sync.dma_start(
-            out=b_rows[0:P:32, :].rearrange("a (j i) -> a j i", i=32),
-            in_=b.rearrange("(j a i) -> a j i", a=4, i=32),
+            out=b_rows[0:P:QUADRANT, :].rearrange("a (j c) -> a j c", c=QUADRANT),
+            in_=b.rearrange("(j a c) -> a j c", a=P // QUADRANT, c=QUADRANT),
         )
-        nc.sync.dma_start(out=x4[:, :T], in_=x4_words[0, :, :T])
-        load_xr(nc.sync, raw_hi, HALF, T)
-        nc.sync.dma_start(out=w4[:, 2048:], in_=w4_words[0, :, 2048:])
-        nc.sync.dma_start(out=x4[:, T:], in_=x4_words[0, :, T:])
-        nc.scalar.activation(out=warm[:, 8:9], in_=warm[:, 0:1], func=IDENTITY)
+        nc.sync.dma_start(out=x4[:, : 2 * HALF], in_=x4_words[0, :, : 2 * HALF])
+        load_xr(raw_hi, HALF, T)
+        nc.sync.dma_start(out=w4[:, w4_cut:], in_=w4_words[0, :, w4_cut:])
+        nc.sync.dma_start(out=x4[:, 2 * HALF :], in_=x4_words[0, :, 2 * HALF :])
 
-        def cast(copy, tile, origin, t0, t1):
-            copy(out=grouped[:, t0:t1, :], in_=tile[:, :, t0 - origin : t1 - origin].rearrange("p j t -> p t j"))
+        def cast(copy, raw, first, t0, t1):
+            copy(
+                out=grouped[:, t0:t1, :].rearrange("p (c d) i -> p c i d", d=4),
+                in_=raw[:, :, t0 - first : t1 - first].rearrange("p i (c d) -> p c i d", d=4),
+            )
+
+        def cast_quarter(raw, first):
+            cast(nc.vector.tensor_copy, raw, first, first, first + VECTOR_SHARE)
+            cast(nc.scalar.copy, raw, first, first + VECTOR_SHARE, first + QUARTER)
 
         def quantize(t0, t1):
             nc.vector.quantize_mx(
-                out=codes[:, t0:t1].bitcast(FP8X4),
-                scales=scales[:, t0:t1],
-                in_=grouped[:, t0:t1, :].rearrange("p t j -> p (t j)"),
+                out=xr_codes[:, t0:t1].bitcast(FP8X4),
+                scales=xr_scale[:, t0:t1],
+                in_=grouped[:, t0:t1, :].rearrange("p t i -> p (t i)"),
             )
 
-        def prepare_quarter(tile, origin):
-            cast(nc.vector.tensor_copy, tile, origin, origin, origin + 160)
-            cast(nc.scalar.copy, tile, origin, origin + 160, origin + QUARTER)
-            quantize(origin, origin + QUARTER)
-
         def prepare_second_half():
-            cast(nc.vector.tensor_copy, raw_hi, HALF, 512, 768)
-            cast(nc.vector.tensor_copy, raw_hi, HALF, 768, 1024)
-            quantize(512, 768)
-            quantize(768, 1024)
+            for t0 in (HALF, HALF + QUARTER):
+                cast(nc.vector.tensor_copy, raw_hi, HALF, t0, t0 + QUARTER)
+            for t0 in (HALF, HALF + QUARTER):
+                quantize(t0, t0 + QUARTER)
 
         banks = {}
 
-        def add_product(unit, t0, t1, rhs, rhs_scale, stop):
+        def add_pass(unit, t0, t1, rhs, rhs_scale, stop):
             j, origin = unit
             start = unit not in banks
             if start:
@@ -113,7 +117,7 @@ def tile_mix_xres_fm_bias_kernel(tc, x4_words, x4_scales, xr, w4_words, w4_scale
             nc.tensor.matmul_mx(
                 out=banks[unit][:, t0 - origin : t1 - origin],
                 lhsT=w4[:, 2 * P * j : 2 * P * (j + 1)].bitcast(FP4X4),
-                lhsT_scale=w4_plane[:, P * j : P * (j + 1)],
+                lhsT_scale=w4_scale[:, P * j : P * (j + 1)],
                 rhs=rhs,
                 rhs_scale=rhs_scale,
                 start=start,
@@ -121,61 +125,77 @@ def tile_mix_xres_fm_bias_kernel(tc, x4_words, x4_scales, xr, w4_words, w4_scale
             )
 
         def add_x4(unit, t0, t1, stop=False):
-            add_product(unit, t0, t1, x4[:, 2 * t0 : 2 * t1].bitcast(FP4X4), x4_plane[:, t0:t1], stop)
+            add_pass(unit, t0, t1, x4[:, 2 * t0 : 2 * t1].bitcast(FP4X4), x4_scale[:, t0:t1], stop)
 
         def add_xr(unit, t0, t1, stop=False):
             step = HALF if t1 - t0 == HALF else P
             for t in range(t0, t1, step):
-                last = stop and t + step == t1
-                add_product(unit, t, t + step, codes[:, t : t + step].bitcast(FP8X4), scales[:, t : t + step], last)
+                cols = slice(t, t + step)
+                add_pass(unit, t, t + step, xr_codes[:, cols].bitcast(FP8X4), xr_scale[:, cols], stop and t + step == t1)
 
-        def drain(unit, on_vector):
-            j, t0 = unit
-            o = result[:, j, t0 : t0 + HALF]
-            bias = b_cols[:, 32 * j : 32 * j + 1]
+        def drain(unit, width, on_vector):
+            j, origin = unit
+            dst = result[:, j, origin : origin + width]
+            acc = banks[unit][:, :width]
+            bias = b_cols[:, QUADRANT * j : QUADRANT * j + 1]
             if on_vector:
-                nc.vector.tensor_scalar(out=o, in0=banks[unit][:], scalar1=bias, scalar2=None, op0=ADD)
+                nc.vector.tensor_scalar(out=dst, in0=acc, scalar1=bias, scalar2=None, op0=ADD)
             else:
-                nc.scalar.activation(out=o, in_=banks[unit][:], func=IDENTITY, bias=bias)
+                nc.scalar.activation(out=dst, in_=acc, func=IDENTITY, bias=bias)
 
         out_tiles = out.rearrange("(j p) t -> p j t", p=P)
 
         def store(j0, j1, t0, t1):
             nc.sync.dma_start(out=out_tiles[:, j0:j1, t0:t1], in_=result[:, j0:j1, t0:t1])
 
-        first_stores = {0: 0, 1: 1, 2: 2, 4: 3, 6: 5}
-        whole_stores = {7: 7, 8: 8, 9: 9, 10: 10, 11: 11}
-        last_stores = {2: 0, 5: 3, 6: 6}
+        quarter_tiles = range(QUARTER_TILES)
+        half_tiles = range(QUARTER_TILES, QUARTER_TILES + HALF_TILES)
+        whole_tiles = range(QUARTER_TILES + HALF_TILES, TILES)
 
-        prepare_quarter(raw_a, 0)
-        for j in range(EARLY):
+        cast_quarter(raw_q0, 0)
+        quantize(0, QUARTER)
+        for j in range(EARLY_TILES):
             add_xr((j, 0), 0, QUARTER)
-        prepare_quarter(raw_b, QUARTER)
-        nc.vector.transpose(b_cols[:, 0:128], b_rows[:, 0:128])
-        nc.vector.transpose(b_cols[:, 128:384], b_rows[:, 128:384])
-        for j in range(SOLO + AHEAD):
-            if j < EARLY:
+
+        cast_quarter(raw_q1, QUARTER)
+        nc.vector.transpose(b_cols[:, :P], b_rows[:, :P])
+        quantize(QUARTER, HALF)
+        nc.vector.transpose(b_cols[:, P:], b_rows[:, P:])
+
+        for j in quarter_tiles:
+            add_x4((j, 0), 0, QUARTER, stop=True)
+            drain((j, 0), QUARTER, False)
+            store(j, j + 1, 0, QUARTER)
+
+        for j in half_tiles:
+            if j < EARLY_TILES:
                 add_x4((j, 0), 0, QUARTER)
                 add_x4((j, 0), QUARTER, HALF)
                 add_xr((j, 0), QUARTER, HALF, stop=True)
             else:
                 add_x4((j, 0), 0, HALF)
                 add_xr((j, 0), 0, HALF, stop=True)
-            if j == 3:
+            drain((j, 0), HALF, j == QUARTER_TILES)
+            store(j, j + 1, 0, HALF)
+            if j == QUARTER_TILES:
                 prepare_second_half()
-            drain((j, 0), j in (0, 2, SOLO + AHEAD - 1))
-            if j in first_stores:
-                store(first_stores[j], j + 1, 0, HALF)
-        units = [(j, HALF) for j in range(SOLO, SOLO + AHEAD)]
-        units += [(j, t0) for j in range(SOLO + AHEAD, TILES) for t0 in (0, HALF)]
-        units += [(j, HALF) for j in range(SOLO)]
+
+        for j in quarter_tiles:
+            add_x4((j, QUARTER), QUARTER, HALF)
+            add_xr((j, QUARTER), QUARTER, HALF, stop=True)
+            drain((j, QUARTER), QUARTER, False)
+
+        units = [(j, HALF) for j in quarter_tiles]
+        units += [(j, t0) for j in whole_tiles for t0 in (0, HALF)]
+        units += [(j, HALF) for j in half_tiles]
         for u, (j, t0) in enumerate(units):
-            for ahead in units[: u + 1 + LEAD]:
-                if ahead not in banks:
-                    add_x4(ahead, ahead[1], ahead[1] + HALF)
+            add_x4((j, t0), t0, t0 + HALF)
             add_xr((j, t0), t0, t0 + HALF, stop=True)
-            drain((j, t0), u % 2 == 1)
-            if t0 == HALF and j in whole_stores:
-                store(whole_stores[j], j + 1, 0, T)
-            if t0 == HALF and j in last_stores:
-                store(last_stores[j], j + 1, HALF, T)
+            drain((j, t0), HALF, u % 2 == 0)
+            if j in quarter_tiles:
+                store(j, j + 1, QUARTER, T)
+            elif j in whole_tiles:
+                if t0 == HALF:
+                    store(j, j + 1, 0, T)
+            elif (j - QUARTER_TILES) % 2 == 1:
+                store(j - 1, j + 1, HALF, T)

@@ -26,9 +26,11 @@ FLOPS = 2 * 2 * K * M * T
 
 QUARTER_TILES = 3
 HALF_TILES = 6
-EARLY_TILES = 4
+EARLY_TILES = 6
 VECTOR_SHARE = 160
 W4_FIRST_TILES = 8
+SINGLE_HALVES = 2
+SECOND_HALF_GROUP = 3
 
 
 def tile_mix_xres_fm_bias_kernel(tc, x4_words, x4_scales, xr, w4_words, w4_scales, b, out):
@@ -90,7 +92,8 @@ def tile_mix_xres_fm_bias_kernel(tc, x4_words, x4_scales, xr, w4_words, w4_scale
             )
 
         def cast_quarter(raw, first):
-            cast(nc.vector.tensor_copy, raw, first, first, first + VECTOR_SHARE)
+            cast(nc.vector.tensor_copy, raw, first, first, first + P)
+            cast(nc.vector.tensor_copy, raw, first, first + P, first + VECTOR_SHARE)
             cast(nc.scalar.copy, raw, first, first + VECTOR_SHARE, first + QUARTER)
 
         def quantize(t0, t1):
@@ -153,13 +156,16 @@ def tile_mix_xres_fm_bias_kernel(tc, x4_words, x4_scales, xr, w4_words, w4_scale
         whole_tiles = range(QUARTER_TILES + HALF_TILES, TILES)
 
         cast_quarter(raw_q0, 0)
-        quantize(0, QUARTER)
-        for j in range(EARLY_TILES):
-            add_xr((j, 0), 0, QUARTER)
+        for t0 in (0, P):
+            quantize(t0, t0 + P)
+        for t0 in (0, P):
+            for j in range(EARLY_TILES):
+                add_xr((j, 0), t0, t0 + P)
 
         cast_quarter(raw_q1, QUARTER)
         nc.vector.transpose(b_cols[:, :P], b_rows[:, :P])
-        quantize(QUARTER, HALF)
+        for t0 in (QUARTER, QUARTER + P):
+            quantize(t0, t0 + P)
         nc.vector.transpose(b_cols[:, P:], b_rows[:, P:])
 
         for j in quarter_tiles:
@@ -169,14 +175,17 @@ def tile_mix_xres_fm_bias_kernel(tc, x4_words, x4_scales, xr, w4_words, w4_scale
 
         for j in half_tiles:
             if j < EARLY_TILES:
-                add_x4((j, 0), 0, QUARTER)
-                add_x4((j, 0), QUARTER, HALF)
-                add_xr((j, 0), QUARTER, HALF, stop=True)
+                add_xr((j, 0), QUARTER, HALF)
+                add_x4((j, 0), 0, HALF, stop=True)
             else:
                 add_x4((j, 0), 0, HALF)
                 add_xr((j, 0), 0, HALF, stop=True)
             drain((j, 0), HALF, j == QUARTER_TILES)
-            store(j, j + 1, 0, HALF)
+            place = j - QUARTER_TILES
+            if place < SINGLE_HALVES:
+                store(j, j + 1, 0, HALF)
+            elif (place - SINGLE_HALVES) % 2 == 1:
+                store(j - 1, j + 1, 0, HALF)
             if j == QUARTER_TILES:
                 prepare_second_half()
 
@@ -197,5 +206,5 @@ def tile_mix_xres_fm_bias_kernel(tc, x4_words, x4_scales, xr, w4_words, w4_scale
             elif j in whole_tiles:
                 if t0 == HALF:
                     store(j, j + 1, 0, T)
-            elif (j - QUARTER_TILES) % 2 == 1:
-                store(j - 1, j + 1, HALF, T)
+            elif (j + 1 - QUARTER_TILES) % SECOND_HALF_GROUP == 0:
+                store(j + 1 - SECOND_HALF_GROUP, j + 1, HALF, T)

@@ -26,11 +26,12 @@ FLOPS = 2 * 2 * K * M * T
 
 QUARTER_TILES = 3
 HALF_TILES = 6
-EARLY_TILES = 6
+EARLY_TILES = 8
 VECTOR_SHARE = 160
 W4_FIRST_TILES = 8
-SINGLE_HALVES = 2
+FIRST_HALF_GROUP = 2
 SECOND_HALF_GROUP = 3
+WARM_PASSES = 4
 
 
 def tile_mix_xres_fm_bias_kernel(tc, x4_words, x4_scales, xr, w4_words, w4_scales, b, out):
@@ -60,6 +61,28 @@ def tile_mix_xres_fm_bias_kernel(tc, x4_words, x4_scales, xr, w4_words, w4_scale
         nc.vector.memset(w4_scale[:].bitcast(I32), 0)
         nc.scalar.activation(out=b_rows[:], in_=zero[:].to_broadcast([P, TILES * QUADRANT]), func=IDENTITY)
 
+        warm_in = keep.tile([P, PACK * QUARTER], BF16, name="warm_in", align_bytes=256)
+        warm_codes = keep.tile([P, HALF], U32, name="warm_codes", align_bytes=256)
+        warm_scale = keep.tile([P, HALF], U8, name="warm_scale", align_bytes=256)
+        nc.vector.memset(warm_in[:].bitcast(I32), 0)
+        for t0 in (0, QUARTER):
+            nc.vector.quantize_mx(
+                out=warm_codes[:, t0 : t0 + QUARTER].bitcast(FP8X4),
+                scales=warm_scale[:, t0 : t0 + QUARTER],
+                in_=warm_in[:],
+            )
+        warm_acc = psum.tile([P, HALF], F32, name="acc")
+        for step in range(WARM_PASSES):
+            nc.tensor.matmul_mx(
+                out=warm_acc[:],
+                lhsT=warm_codes[:, : P // 2].bitcast(FP4X4),
+                lhsT_scale=warm_scale[:, :P],
+                rhs=warm_codes[:].bitcast(FP8X4),
+                rhs_scale=warm_scale[:],
+                start=step == 0,
+                stop=step == WARM_PASSES - 1,
+            )
+
         def load_scale_rows(queue, scale, rows, r):
             queue.dma_start(out=scale[r:P:QUADRANT, :].bitcast(I32), in_=rows[0, r:16:4, :].bitcast(I32))
 
@@ -76,11 +99,11 @@ def tile_mix_xres_fm_bias_kernel(tc, x4_words, x4_scales, xr, w4_words, w4_scale
         load_xr(raw_q1, QUARTER, HALF)
         for r in range(2, 4):
             load_scale_rows(nc.sync, x4_scale, x4_scales, r)
+        nc.sync.dma_start(out=x4[:, : 2 * HALF], in_=x4_words[0, :, : 2 * HALF])
         nc.sync.dma_start(
             out=b_rows[0:P:QUADRANT, :].rearrange("a (j c) -> a j c", c=QUADRANT),
             in_=b.rearrange("(j a c) -> a j c", a=P // QUADRANT, c=QUADRANT),
         )
-        nc.sync.dma_start(out=x4[:, : 2 * HALF], in_=x4_words[0, :, : 2 * HALF])
         load_xr(raw_hi, HALF, T)
         nc.sync.dma_start(out=w4[:, w4_cut:], in_=w4_words[0, :, w4_cut:])
         nc.sync.dma_start(out=x4[:, 2 * HALF :], in_=x4_words[0, :, 2 * HALF :])
@@ -131,10 +154,7 @@ def tile_mix_xres_fm_bias_kernel(tc, x4_words, x4_scales, xr, w4_words, w4_scale
             add_pass(unit, t0, t1, x4[:, 2 * t0 : 2 * t1].bitcast(FP4X4), x4_scale[:, t0:t1], stop)
 
         def add_xr(unit, t0, t1, stop=False):
-            step = HALF if t1 - t0 == HALF else P
-            for t in range(t0, t1, step):
-                cols = slice(t, t + step)
-                add_pass(unit, t, t + step, xr_codes[:, cols].bitcast(FP8X4), xr_scale[:, cols], stop and t + step == t1)
+            add_pass(unit, t0, t1, xr_codes[:, t0:t1].bitcast(FP8X4), xr_scale[:, t0:t1], stop)
 
         def drain(unit, width, on_vector):
             j, origin = unit
@@ -163,15 +183,15 @@ def tile_mix_xres_fm_bias_kernel(tc, x4_words, x4_scales, xr, w4_words, w4_scale
                 add_xr((j, 0), t0, t0 + P)
 
         cast_quarter(raw_q1, QUARTER)
-        nc.vector.transpose(b_cols[:, :P], b_rows[:, :P])
         for t0 in (QUARTER, QUARTER + P):
             quantize(t0, t0 + P)
+        nc.vector.transpose(b_cols[:, :P], b_rows[:, :P])
         nc.vector.transpose(b_cols[:, P:], b_rows[:, P:])
 
         for j in quarter_tiles:
             add_x4((j, 0), 0, QUARTER, stop=True)
-            drain((j, 0), QUARTER, False)
-            store(j, j + 1, 0, QUARTER)
+            drain((j, 0), QUARTER, j % 2 == 1)
+        store(0, QUARTER_TILES, 0, QUARTER)
 
         for j in half_tiles:
             if j < EARLY_TILES:
@@ -181,11 +201,8 @@ def tile_mix_xres_fm_bias_kernel(tc, x4_words, x4_scales, xr, w4_words, w4_scale
                 add_x4((j, 0), 0, HALF)
                 add_xr((j, 0), 0, HALF, stop=True)
             drain((j, 0), HALF, j == QUARTER_TILES)
-            place = j - QUARTER_TILES
-            if place < SINGLE_HALVES:
-                store(j, j + 1, 0, HALF)
-            elif (place - SINGLE_HALVES) % 2 == 1:
-                store(j - 1, j + 1, 0, HALF)
+            if (j + 1 - QUARTER_TILES) % FIRST_HALF_GROUP == 0:
+                store(j + 1 - FIRST_HALF_GROUP, j + 1, 0, HALF)
             if j == QUARTER_TILES:
                 prepare_second_half()
 
@@ -195,14 +212,15 @@ def tile_mix_xres_fm_bias_kernel(tc, x4_words, x4_scales, xr, w4_words, w4_scale
             drain((j, QUARTER), QUARTER, False)
 
         units = [(j, HALF) for j in quarter_tiles]
-        units += [(j, t0) for j in whole_tiles for t0 in (0, HALF)]
         units += [(j, HALF) for j in half_tiles]
+        units += [(j, t0) for j in whole_tiles for t0 in (0, HALF)]
         for u, (j, t0) in enumerate(units):
             add_x4((j, t0), t0, t0 + HALF)
             add_xr((j, t0), t0, t0 + HALF, stop=True)
             drain((j, t0), HALF, u % 2 == 0)
             if j in quarter_tiles:
-                store(j, j + 1, QUARTER, T)
+                if j % 2 == 0:
+                    store(max(j - 1, 0), j + 1, QUARTER, T)
             elif j in whole_tiles:
                 if t0 == HALF:
                     store(j, j + 1, 0, T)

@@ -29,7 +29,7 @@ HALF_TILES = 6
 EARLY_TILES = 8
 VECTOR_SHARE = 160
 W4_FIRST_TILES = 8
-FIRST_HALF_GROUP = 2
+SINGLE_HALVES = 2
 SECOND_HALF_GROUP = 3
 WARM_PASSES = 4
 
@@ -56,7 +56,6 @@ def tile_mix_xres_fm_bias_kernel(tc, x4_words, x4_scales, xr, w4_words, w4_scale
         result = keep.tile([P, TILES, T], F32, name="result", align_bytes=256)
         zero = keep.tile([P, 1], F32, name="zero", align_bytes=256)
 
-        nc.gpsimd.memset(x4_scale[:].bitcast(I32), 0)
         nc.vector.memset(zero[:], 0.0)
         nc.vector.memset(w4_scale[:].bitcast(I32), 0)
         nc.scalar.activation(out=b_rows[:], in_=zero[:].to_broadcast([P, TILES * QUADRANT]), func=IDENTITY)
@@ -71,6 +70,7 @@ def tile_mix_xres_fm_bias_kernel(tc, x4_words, x4_scales, xr, w4_words, w4_scale
                 scales=warm_scale[:, t0 : t0 + QUARTER],
                 in_=warm_in[:],
             )
+        nc.vector.memset(x4_scale[:].bitcast(I32), 0)
         warm_acc = psum.tile([P, HALF], F32, name="acc")
         for step in range(WARM_PASSES):
             nc.tensor.matmul_mx(
@@ -91,19 +91,17 @@ def tile_mix_xres_fm_bias_kernel(tc, x4_words, x4_scales, xr, w4_words, w4_scale
 
         w4_cut = 2 * P * W4_FIRST_TILES
         load_xr(raw_q0, 0, QUARTER)
-        for r in range(2):
-            load_scale_rows(nc.gpsimd, x4_scale, x4_scales, r)
         for r in range(4):
             load_scale_rows(nc.sync, w4_scale, w4_scales, r)
         nc.sync.dma_start(out=w4[:, :w4_cut], in_=w4_words[0, :, :w4_cut])
         load_xr(raw_q1, QUARTER, HALF)
-        for r in range(2, 4):
+        for r in range(4):
             load_scale_rows(nc.sync, x4_scale, x4_scales, r)
-        nc.sync.dma_start(out=x4[:, : 2 * HALF], in_=x4_words[0, :, : 2 * HALF])
         nc.sync.dma_start(
             out=b_rows[0:P:QUADRANT, :].rearrange("a (j c) -> a j c", c=QUADRANT),
             in_=b.rearrange("(j a c) -> a j c", a=P // QUADRANT, c=QUADRANT),
         )
+        nc.sync.dma_start(out=x4[:, : 2 * HALF], in_=x4_words[0, :, : 2 * HALF])
         load_xr(raw_hi, HALF, T)
         nc.sync.dma_start(out=w4[:, w4_cut:], in_=w4_words[0, :, w4_cut:])
         nc.sync.dma_start(out=x4[:, 2 * HALF :], in_=x4_words[0, :, 2 * HALF :])
@@ -183,15 +181,16 @@ def tile_mix_xres_fm_bias_kernel(tc, x4_words, x4_scales, xr, w4_words, w4_scale
                 add_xr((j, 0), t0, t0 + P)
 
         cast_quarter(raw_q1, QUARTER)
+        nc.vector.transpose(b_cols[:, :P], b_rows[:, :P])
         for t0 in (QUARTER, QUARTER + P):
             quantize(t0, t0 + P)
-        nc.vector.transpose(b_cols[:, :P], b_rows[:, :P])
         nc.vector.transpose(b_cols[:, P:], b_rows[:, P:])
 
         for j in quarter_tiles:
             add_x4((j, 0), 0, QUARTER, stop=True)
             drain((j, 0), QUARTER, j % 2 == 1)
-        store(0, QUARTER_TILES, 0, QUARTER)
+            if j % 2 == 0:
+                store(max(j - 1, 0), j + 1, 0, QUARTER)
 
         for j in half_tiles:
             if j < EARLY_TILES:
@@ -201,8 +200,11 @@ def tile_mix_xres_fm_bias_kernel(tc, x4_words, x4_scales, xr, w4_words, w4_scale
                 add_x4((j, 0), 0, HALF)
                 add_xr((j, 0), 0, HALF, stop=True)
             drain((j, 0), HALF, j == QUARTER_TILES)
-            if (j + 1 - QUARTER_TILES) % FIRST_HALF_GROUP == 0:
-                store(j + 1 - FIRST_HALF_GROUP, j + 1, 0, HALF)
+            place = j - QUARTER_TILES
+            if place < SINGLE_HALVES:
+                store(j, j + 1, 0, HALF)
+            elif (place - SINGLE_HALVES) % 2 == 1:
+                store(j - 1, j + 1, 0, HALF)
             if j == QUARTER_TILES:
                 prepare_second_half()
 
@@ -219,8 +221,7 @@ def tile_mix_xres_fm_bias_kernel(tc, x4_words, x4_scales, xr, w4_words, w4_scale
             add_xr((j, t0), t0, t0 + HALF, stop=True)
             drain((j, t0), HALF, u % 2 == 0)
             if j in quarter_tiles:
-                if j % 2 == 0:
-                    store(max(j - 1, 0), j + 1, QUARTER, T)
+                store(j, j + 1, QUARTER, T)
             elif j in whole_tiles:
                 if t0 == HALF:
                     store(j, j + 1, 0, T)

@@ -6,6 +6,7 @@ F32 = mybir.dt.float32
 BF16 = mybir.dt.bfloat16
 U32 = mybir.dt.uint32
 I32 = mybir.dt.int32
+U16 = mybir.dt.uint16
 U8 = mybir.dt.uint8
 FP8X4 = mybir.dt.float8_e4m3fn_x4
 FP4X4 = mybir.dt.float4_e2m1fn_x4
@@ -25,11 +26,12 @@ QUADRANT = 32
 FLOPS = 2 * 2 * K * M * T
 
 QUARTER_TILES = 3
-HALF_TILES = 6
+HALF_TILES = 5
 EARLY_TILES = 8
 VECTOR_SHARE = 160
 W4_FIRST_TILES = 8
-SINGLE_HALVES = 2
+PLAIN = P * W4_FIRST_TILES
+SINGLE_HALVES = 1
 SECOND_HALF_GROUP = 3
 WARM_PASSES = 4
 
@@ -43,6 +45,9 @@ def tile_mix_xres_fm_bias_kernel(tc, x4_words, x4_scales, xr, w4_words, w4_scale
 
         w4 = keep.tile([P, 2 * M], U8, name="w4", align_bytes=256)
         w4_scale = keep.tile([P, M], U8, name="w4_scale", align_bytes=256)
+        w4_late = keep.tile([P, 2 * (M - PLAIN)], U8, name="w4_late", align_bytes=256)
+        pair_scale = keep.tile([P, M - PLAIN], U8, name="pair_scale", align_bytes=256)
+        b_pairs = keep.tile([P, P], F32, name="b_pairs", align_bytes=256)
         x4 = keep.tile([P, 2 * T], U8, name="x4", align_bytes=256)
         x4_scale = keep.tile([P, T], U8, name="x4_scale", align_bytes=256)
         xr_codes = keep.tile([P, T], U32, name="xr_codes", align_bytes=256)
@@ -90,6 +95,7 @@ def tile_mix_xres_fm_bias_kernel(tc, x4_words, x4_scales, xr, w4_words, w4_scale
             nc.sync.dma_start(out=raw[:], in_=xr[:, t0:t1].rearrange("(p i) t -> p i t", i=PACK))
 
         w4_cut = 2 * P * W4_FIRST_TILES
+        b_cut = QUADRANT * W4_FIRST_TILES
         load_xr(raw_q0, 0, QUARTER)
         for r in range(4):
             load_scale_rows(nc.sync, w4_scale, w4_scales, r)
@@ -98,13 +104,17 @@ def tile_mix_xres_fm_bias_kernel(tc, x4_words, x4_scales, xr, w4_words, w4_scale
         for r in range(4):
             load_scale_rows(nc.sync, x4_scale, x4_scales, r)
         nc.sync.dma_start(
-            out=b_rows[0:P:QUADRANT, :].rearrange("a (j c) -> a j c", c=QUADRANT),
-            in_=b.rearrange("(j a c) -> a j c", a=P // QUADRANT, c=QUADRANT),
+            out=b_rows[0:P:QUADRANT, :b_cut].rearrange("a (j c) -> a j c", c=QUADRANT),
+            in_=b[:PLAIN].rearrange("(j a c) -> a j c", a=P // QUADRANT, c=QUADRANT),
         )
         nc.sync.dma_start(out=x4[:, : 2 * HALF], in_=x4_words[0, :, : 2 * HALF])
         load_xr(raw_hi, HALF, T)
-        nc.sync.dma_start(out=w4[:, w4_cut:], in_=w4_words[0, :, w4_cut:])
+        nc.sync.dma_start(out=w4_late[:], in_=w4_words[0, :, w4_cut:])
         nc.sync.dma_start(out=x4[:, 2 * HALF :], in_=x4_words[0, :, 2 * HALF :])
+        nc.sync.dma_start(
+            out=b_rows[0:P:QUADRANT, b_cut:].rearrange("a (g e) -> a g e", e=2 * QUADRANT),
+            in_=b[PLAIN:].rearrange("(g a e) -> a g e", a=P // QUADRANT, e=2 * QUADRANT),
+        )
 
         def cast(copy, raw, first, t0, t1):
             copy(
@@ -141,7 +151,7 @@ def tile_mix_xres_fm_bias_kernel(tc, x4_words, x4_scales, xr, w4_words, w4_scale
             nc.tensor.matmul_mx(
                 out=banks[unit][:, t0 - origin : t1 - origin],
                 lhsT=w4[:, 2 * P * j : 2 * P * (j + 1)].bitcast(FP4X4),
-                lhsT_scale=w4_scale[:, P * j : P * (j + 1)],
+                lhsT_scale=w4_scale[:, P * j : P * (j + 1)] if P * j < PLAIN else pair_scale[:, P * j - PLAIN : P * (j + 1) - PLAIN],
                 rhs=rhs,
                 rhs_scale=rhs_scale,
                 start=start,
@@ -180,11 +190,15 @@ def tile_mix_xres_fm_bias_kernel(tc, x4_words, x4_scales, xr, w4_words, w4_scale
             for j in range(EARLY_TILES):
                 add_xr((j, 0), t0, t0 + P)
 
+        nc.vector.tensor_copy(
+            out=pair_scale[:].rearrange("k (g i p) -> k g p i", i=2, p=P),
+            in_=w4_scale[:, PLAIN:].rearrange("k (g p i) -> k g p i", i=2, p=P),
+        )
         cast_quarter(raw_q1, QUARTER)
         nc.vector.transpose(b_cols[:, :P], b_rows[:, :P])
         for t0 in (QUARTER, QUARTER + P):
             quantize(t0, t0 + P)
-        nc.vector.transpose(b_cols[:, P:], b_rows[:, P:])
+        nc.vector.transpose(b_cols[:, P:b_cut], b_rows[:, P:b_cut])
 
         for j in quarter_tiles:
             add_x4((j, 0), 0, QUARTER, stop=True)
@@ -213,17 +227,44 @@ def tile_mix_xres_fm_bias_kernel(tc, x4_words, x4_scales, xr, w4_words, w4_scale
             add_xr((j, QUARTER), QUARTER, HALF, stop=True)
             drain((j, QUARTER), QUARTER, False)
 
-        units = [(j, HALF) for j in quarter_tiles]
-        units += [(j, HALF) for j in half_tiles]
+        def deal_columns(g):
+            nc.scalar.copy(
+                out=w4[:, w4_cut + 4 * P * g : w4_cut + 4 * P * (g + 1)].bitcast(U16).rearrange("k (i p) -> k i p", i=2),
+                in_=w4_late[:, 4 * P * g : 4 * P * (g + 1)].bitcast(U16).rearrange("k (p i) -> k i p", i=2),
+            )
+
+        def deal_bias():
+            nc.vector.tensor_copy(
+                out=b_pairs[:].rearrange("a (g i c) -> a g i c", i=2, c=QUADRANT),
+                in_=b_rows[:, b_cut:].rearrange("a (g c i) -> a g i c", i=2, c=QUADRANT),
+            )
+
+        late_halves = range(QUARTER_TILES + SECOND_HALF_GROUP, QUARTER_TILES + HALF_TILES)
+        units = [(j, HALF) for j in range(QUARTER_TILES + SECOND_HALF_GROUP)]
         units += [(j, t0) for j in whole_tiles for t0 in (0, HALF)]
+        units += [(j, HALF) for j in late_halves]
+        for j in quarter_tiles:
+            add_x4((j, HALF), HALF, T)
         for u, (j, t0) in enumerate(units):
-            add_x4((j, t0), t0, t0 + HALF)
+            if j not in quarter_tiles:
+                add_x4((j, t0), t0, t0 + HALF)
             add_xr((j, t0), t0, t0 + HALF, stop=True)
             drain((j, t0), HALF, u % 2 == 0)
+            if u == 0:
+                deal_bias()
+            if u == 2:
+                nc.vector.transpose(b_cols[:, b_cut:], b_pairs[:])
+            if u in (1, 3):
+                deal_columns(u // 2)
             if j in quarter_tiles:
                 store(j, j + 1, QUARTER, T)
             elif j in whole_tiles:
-                if t0 == HALF:
-                    store(j, j + 1, 0, T)
-            elif (j + 1 - QUARTER_TILES) % SECOND_HALF_GROUP == 0:
-                store(j + 1 - SECOND_HALF_GROUP, j + 1, HALF, T)
+                if t0 == HALF and j % 2 == 1:
+                    nc.sync.dma_start(
+                        out=out[P * (j - 1) : P * (j + 1), :].rearrange("(p i) t -> p (i t)", i=2),
+                        in_=result[:, j - 1 : j + 1, :].rearrange("p i t -> p (i t)"),
+                    )
+            elif j + 1 == late_halves.start:
+                store(QUARTER_TILES, j + 1, HALF, T)
+            elif j + 1 == late_halves.stop:
+                store(late_halves.start, j + 1, HALF, T)

@@ -103,11 +103,11 @@ def tile_mix_xres_fm_bias_kernel(tc, x4_words, x4_scales, xr, w4_words, w4_scale
         load_xr(raw_q1, QUARTER, HALF)
         for r in range(4):
             load_scale_rows(nc.sync, x4_scale, x4_scales, r)
+        nc.sync.dma_start(out=x4[:, : 2 * HALF], in_=x4_words[0, :, : 2 * HALF])
         nc.sync.dma_start(
             out=b_rows[0:P:QUADRANT, :b_cut].rearrange("a (j c) -> a j c", c=QUADRANT),
             in_=b[:PLAIN].rearrange("(j a c) -> a j c", a=P // QUADRANT, c=QUADRANT),
         )
-        nc.sync.dma_start(out=x4[:, : 2 * HALF], in_=x4_words[0, :, : 2 * HALF])
         load_xr(raw_hi, HALF, T)
         nc.sync.dma_start(out=w4_late[:], in_=w4_words[0, :, w4_cut:])
         nc.sync.dma_start(out=x4[:, 2 * HALF :], in_=x4_words[0, :, 2 * HALF :])
@@ -121,11 +121,6 @@ def tile_mix_xres_fm_bias_kernel(tc, x4_words, x4_scales, xr, w4_words, w4_scale
                 out=grouped[:, t0:t1, :].rearrange("p (c d) i -> p c i d", d=4),
                 in_=raw[:, :, t0 - first : t1 - first].rearrange("p i (c d) -> p c i d", d=4),
             )
-
-        def cast_quarter(raw, first):
-            cast(nc.vector.tensor_copy, raw, first, first, first + P)
-            cast(nc.vector.tensor_copy, raw, first, first + P, first + VECTOR_SHARE)
-            cast(nc.scalar.copy, raw, first, first + VECTOR_SHARE, first + QUARTER)
 
         def quantize(t0, t1):
             nc.vector.quantize_mx(
@@ -183,7 +178,9 @@ def tile_mix_xres_fm_bias_kernel(tc, x4_words, x4_scales, xr, w4_words, w4_scale
         half_tiles = range(QUARTER_TILES, QUARTER_TILES + HALF_TILES)
         whole_tiles = range(QUARTER_TILES + HALF_TILES, TILES)
 
-        cast_quarter(raw_q0, 0)
+        cast(nc.vector.tensor_copy, raw_q0, 0, 0, P)
+        cast(nc.vector.tensor_copy, raw_q0, 0, P, VECTOR_SHARE)
+        cast(nc.scalar.copy, raw_q0, 0, VECTOR_SHARE, QUARTER)
         for t0 in (0, P):
             quantize(t0, t0 + P)
         for t0 in (0, P):
@@ -191,23 +188,29 @@ def tile_mix_xres_fm_bias_kernel(tc, x4_words, x4_scales, xr, w4_words, w4_scale
                 add_xr((j, 0), t0, t0 + P)
 
         nc.vector.tensor_copy(
-            out=pair_scale[:].rearrange("k (g i p) -> k g p i", i=2, p=P),
-            in_=w4_scale[:, PLAIN:].rearrange("k (g p i) -> k g p i", i=2, p=P),
+            out=pair_scale[:].rearrange("k (g i p) -> k g i p", i=2, p=P),
+            in_=w4_scale[:, PLAIN:].rearrange("k (g p i) -> k g i p", i=2, p=P),
         )
-        cast_quarter(raw_q1, QUARTER)
-        nc.vector.transpose(b_cols[:, :P], b_rows[:, :P])
+        for t0 in (QUARTER, QUARTER + P):
+            cast(nc.vector.tensor_copy, raw_q1, QUARTER, t0, t0 + P)
         for t0 in (QUARTER, QUARTER + P):
             quantize(t0, t0 + P)
-        nc.vector.transpose(b_cols[:, P:b_cut], b_rows[:, P:b_cut])
+        nc.vector.transpose(b_cols[:, :P], b_rows[:, :P])
 
         for j in quarter_tiles:
             add_x4((j, 0), 0, QUARTER, stop=True)
-            drain((j, 0), QUARTER, j % 2 == 1)
+            drain((j, 0), QUARTER, j % 2 == 0)
+            if j == 0:
+                nc.vector.transpose(b_cols[:, P:b_cut], b_rows[:, P:b_cut])
             if j % 2 == 0:
                 store(max(j - 1, 0), j + 1, 0, QUARTER)
 
         for j in half_tiles:
-            if j < EARLY_TILES:
+            if j == QUARTER_TILES:
+                add_x4((j, 0), 0, QUARTER)
+                add_x4((j, 0), QUARTER, HALF)
+                add_xr((j, 0), QUARTER, HALF, stop=True)
+            elif j < EARLY_TILES:
                 add_xr((j, 0), QUARTER, HALF)
                 add_x4((j, 0), 0, HALF, stop=True)
             else:
@@ -243,13 +246,21 @@ def tile_mix_xres_fm_bias_kernel(tc, x4_words, x4_scales, xr, w4_words, w4_scale
         units = [(j, HALF) for j in range(QUARTER_TILES + SECOND_HALF_GROUP)]
         units += [(j, t0) for j in whole_tiles for t0 in (0, HALF)]
         units += [(j, HALF) for j in late_halves]
-        for j in quarter_tiles:
+        last_quarters = (HALF, HALF + QUARTER)
+        for t0 in last_quarters:
+            add_x4((0, t0), t0, t0 + QUARTER)
+        for j in quarter_tiles[1:]:
             add_x4((j, HALF), HALF, T)
         for u, (j, t0) in enumerate(units):
-            if j not in quarter_tiles:
-                add_x4((j, t0), t0, t0 + HALF)
-            add_xr((j, t0), t0, t0 + HALF, stop=True)
-            drain((j, t0), HALF, u % 2 == 0)
+            if u == 0:
+                for t1 in last_quarters:
+                    add_xr((0, t1), t1, t1 + QUARTER, stop=True)
+                    drain((0, t1), QUARTER, t1 == HALF)
+            else:
+                if j not in quarter_tiles:
+                    add_x4((j, t0), t0, t0 + HALF)
+                add_xr((j, t0), t0, t0 + HALF, stop=True)
+                drain((j, t0), HALF, u % 2 == 0)
             if u == 0:
                 deal_bias()
             if u == 2:

@@ -31,7 +31,7 @@ EARLY_TILES = 8
 VECTOR_SHARE = 160
 W4_FIRST_TILES = 8
 PLAIN = P * W4_FIRST_TILES
-SINGLE_HALVES = 1
+SINGLE_HALVES = 3
 SECOND_HALF_GROUP = 3
 WARM_PASSES = 4
 
@@ -202,8 +202,7 @@ def tile_mix_xres_fm_bias_kernel(tc, x4_words, x4_scales, xr, w4_words, w4_scale
             drain((j, 0), QUARTER, j % 2 == 0)
             if j == 0:
                 nc.vector.transpose(b_cols[:, P:b_cut], b_rows[:, P:b_cut])
-            if j % 2 == 0:
-                store(max(j - 1, 0), j + 1, 0, QUARTER)
+            store(j, j + 1, 0, QUARTER)
 
         for j in half_tiles:
             if j == QUARTER_TILES:

from contextlib import ExitStack

import concourse.mybir as mybir

F32 = mybir.dt.float32
BF16 = mybir.dt.bfloat16
U32 = mybir.dt.uint32
I32 = mybir.dt.int32
U16 = mybir.dt.uint16
U8 = mybir.dt.uint8
FP8X4 = mybir.dt.float8_e4m3fn_x4
FP4X4 = mybir.dt.float4_e2m1fn_x4
ADD = mybir.AluOpType.add
IDENTITY = mybir.ActivationFunctionType.Identity

P = 128
PACK = 4
K = P * PACK
M = 1536
T = 1024
HALF = T // 2
QUARTER = T // 4
TILES = M // P
BANKS = 8
QUADRANT = 32
FLOPS = 2 * 2 * K * M * T

QUARTER_TILES = 3
HALF_TILES = 5
EARLY_TILES = 8
VECTOR_SHARE = 160
W4_FIRST_TILES = 8
PLAIN = P * W4_FIRST_TILES
SINGLE_HALVES = 3
SECOND_HALF_GROUP = 3
WARM_PASSES = 4


def tile_mix_xres_fm_bias_kernel(tc, x4_words, x4_scales, xr, w4_words, w4_scales, b, out):
    nc = tc.nc
    with ExitStack() as ctx:
        keep = ctx.enter_context(tc.tile_pool(name="keep", bufs=1))
        psum = ctx.enter_context(tc.psum_pool(name="psum", bufs=BANKS))
        ctx.enter_context(tc.manual_schedule())

        w4 = keep.tile([P, 2 * M], U8, name="w4", align_bytes=256)
        w4_scale = keep.tile([P, M], U8, name="w4_scale", align_bytes=256)
        w4_late = keep.tile([P, 2 * (M - PLAIN)], U8, name="w4_late", align_bytes=256)
        pair_scale = keep.tile([P, M - PLAIN], U8, name="pair_scale", align_bytes=256)
        b_pairs = keep.tile([P, P], F32, name="b_pairs", align_bytes=256)
        x4 = keep.tile([P, 2 * T], U8, name="x4", align_bytes=256)
        x4_scale = keep.tile([P, T], U8, name="x4_scale", align_bytes=256)
        xr_codes = keep.tile([P, T], U32, name="xr_codes", align_bytes=256)
        xr_scale = keep.tile([P, T], U8, name="xr_scale", align_bytes=256)
        raw_q0 = keep.tile([P, PACK, QUARTER], F32, name="raw_q0", align_bytes=256)
        raw_q1 = keep.tile([P, PACK, QUARTER], F32, name="raw_q1", align_bytes=256)
        raw_hi = keep.tile([P, PACK, HALF], F32, name="raw_hi", align_bytes=256)
        grouped = keep.tile([P, T, PACK], BF16, name="grouped", align_bytes=256)
        b_rows = keep.tile([P, TILES * QUADRANT], F32, name="b_rows", align_bytes=256)
        b_cols = keep.tile([P, TILES * QUADRANT], F32, name="b_cols", align_bytes=256)
        result = keep.tile([P, TILES, T], F32, name="result", align_bytes=256)
        zero = keep.tile([P, 1], F32, name="zero", align_bytes=256)

        nc.vector.memset(zero[:], 0.0)
        nc.vector.memset(w4_scale[:].bitcast(I32), 0)
        nc.scalar.activation(out=b_rows[:], in_=zero[:].to_broadcast([P, TILES * QUADRANT]), func=IDENTITY)

        warm_in = keep.tile([P, PACK * QUARTER], BF16, name="warm_in", align_bytes=256)
        warm_codes = keep.tile([P, HALF], U32, name="warm_codes", align_bytes=256)
        warm_scale = keep.tile([P, HALF], U8, name="warm_scale", align_bytes=256)
        nc.vector.memset(warm_in[:].bitcast(I32), 0)
        for t0 in (0, QUARTER):
            nc.vector.quantize_mx(
                out=warm_codes[:, t0 : t0 + QUARTER].bitcast(FP8X4),
                scales=warm_scale[:, t0 : t0 + QUARTER],
                in_=warm_in[:],
            )
        nc.vector.memset(x4_scale[:].bitcast(I32), 0)
        warm_acc = psum.tile([P, HALF], F32, name="acc")
        for step in range(WARM_PASSES):
            nc.tensor.matmul_mx(
                out=warm_acc[:],
                lhsT=warm_codes[:, : P // 2].bitcast(FP4X4),
                lhsT_scale=warm_scale[:, :P],
                rhs=warm_codes[:].bitcast(FP8X4),
                rhs_scale=warm_scale[:],
                start=step == 0,
                stop=step == WARM_PASSES - 1,
            )

        def load_scale_rows(queue, scale, rows, r):
            queue.dma_start(out=scale[r:P:QUADRANT, :].bitcast(I32), in_=rows[0, r:16:4, :].bitcast(I32))

        def load_xr(raw, t0, t1):
            nc.sync.dma_start(out=raw[:], in_=xr[:, t0:t1].rearrange("(p i) t -> p i t", i=PACK))

        w4_cut = 2 * P * W4_FIRST_TILES
        b_cut = QUADRANT * W4_FIRST_TILES
        load_xr(raw_q0, 0, QUARTER)
        for r in range(4):
            load_scale_rows(nc.sync, w4_scale, w4_scales, r)
        nc.sync.dma_start(out=w4[:, :w4_cut], in_=w4_words[0, :, :w4_cut])
        load_xr(raw_q1, QUARTER, HALF)
        for r in range(4):
            load_scale_rows(nc.sync, x4_scale, x4_scales, r)
        nc.sync.dma_start(out=x4[:, : 2 * HALF], in_=x4_words[0, :, : 2 * HALF])
        nc.sync.dma_start(
            out=b_rows[0:P:QUADRANT, :b_cut].rearrange("a (j c) -> a j c", c=QUADRANT),
            in_=b[:PLAIN].rearrange("(j a c) -> a j c", a=P // QUADRANT, c=QUADRANT),
        )
        load_xr(raw_hi, HALF, T)
        nc.sync.dma_start(out=w4_late[:], in_=w4_words[0, :, w4_cut:])
        nc.sync.dma_start(out=x4[:, 2 * HALF :], in_=x4_words[0, :, 2 * HALF :])
        nc.sync.dma_start(
            out=b_rows[0:P:QUADRANT, b_cut:].rearrange("a (g e) -> a g e", e=2 * QUADRANT),
            in_=b[PLAIN:].rearrange("(g a e) -> a g e", a=P // QUADRANT, e=2 * QUADRANT),
        )

        def cast(copy, raw, first, t0, t1):
            copy(
                out=grouped[:, t0:t1, :].rearrange("p (c d) i -> p c i d", d=4),
                in_=raw[:, :, t0 - first : t1 - first].rearrange("p i (c d) -> p c i d", d=4),
            )

        def quantize(t0, t1):
            nc.vector.quantize_mx(
                out=xr_codes[:, t0:t1].bitcast(FP8X4),
                scales=xr_scale[:, t0:t1],
                in_=grouped[:, t0:t1, :].rearrange("p t i -> p (t i)"),
            )

        def prepare_second_half():
            for t0 in (HALF, HALF + QUARTER):
                cast(nc.vector.tensor_copy, raw_hi, HALF, t0, t0 + QUARTER)
            for t0 in (HALF, HALF + QUARTER):
                quantize(t0, t0 + QUARTER)

        banks = {}

        def add_pass(unit, t0, t1, rhs, rhs_scale, stop):
            j, origin = unit
            start = unit not in banks
            if start:
                acc = psum.tile([P, HALF], F32, name="acc")
                banks[unit] = acc
            nc.tensor.matmul_mx(
                out=banks[unit][:, t0 - origin : t1 - origin],
                lhsT=w4[:, 2 * P * j : 2 * P * (j + 1)].bitcast(FP4X4),
                lhsT_scale=w4_scale[:, P * j : P * (j + 1)] if P * j < PLAIN else pair_scale[:, P * j - PLAIN : P * (j + 1) - PLAIN],
                rhs=rhs,
                rhs_scale=rhs_scale,
                start=start,
                stop=stop,
            )

        def add_x4(unit, t0, t1, stop=False):
            add_pass(unit, t0, t1, x4[:, 2 * t0 : 2 * t1].bitcast(FP4X4), x4_scale[:, t0:t1], stop)

        def add_xr(unit, t0, t1, stop=False):
            add_pass(unit, t0, t1, xr_codes[:, t0:t1].bitcast(FP8X4), xr_scale[:, t0:t1], stop)

        def drain(unit, width, on_vector):
            j, origin = unit
            dst = result[:, j, origin : origin + width]
            acc = banks[unit][:, :width]
            bias = b_cols[:, QUADRANT * j : QUADRANT * j + 1]
            if on_vector:
                nc.vector.tensor_scalar(out=dst, in0=acc, scalar1=bias, scalar2=None, op0=ADD)
            else:
                nc.scalar.activation(out=dst, in_=acc, func=IDENTITY, bias=bias)

        out_tiles = out.rearrange("(j p) t -> p j t", p=P)

        def store(j0, j1, t0, t1):
            nc.sync.dma_start(out=out_tiles[:, j0:j1, t0:t1], in_=result[:, j0:j1, t0:t1])

        quarter_tiles = range(QUARTER_TILES)
        half_tiles = range(QUARTER_TILES, QUARTER_TILES + HALF_TILES)
        whole_tiles = range(QUARTER_TILES + HALF_TILES, TILES)

        cast(nc.vector.tensor_copy, raw_q0, 0, 0, P)
        cast(nc.vector.tensor_copy, raw_q0, 0, P, VECTOR_SHARE)
        cast(nc.scalar.copy, raw_q0, 0, VECTOR_SHARE, QUARTER)
        for t0 in (0, P):
            quantize(t0, t0 + P)
        for t0 in (0, P):
            for j in range(EARLY_TILES):
                add_xr((j, 0), t0, t0 + P)

        nc.vector.tensor_copy(
            out=pair_scale[:].rearrange("k (g i p) -> k g i p", i=2, p=P),
            in_=w4_scale[:, PLAIN:].rearrange("k (g p i) -> k g i p", i=2, p=P),
        )
        for t0 in (QUARTER, QUARTER + P):
            cast(nc.vector.tensor_copy, raw_q1, QUARTER, t0, t0 + P)
        for t0 in (QUARTER, QUARTER + P):
            quantize(t0, t0 + P)
        nc.vector.transpose(b_cols[:, :P], b_rows[:, :P])

        for j in quarter_tiles:
            add_x4((j, 0), 0, QUARTER, stop=True)
            drain((j, 0), QUARTER, j % 2 == 0)
            if j == 0:
                nc.vector.transpose(b_cols[:, P:b_cut], b_rows[:, P:b_cut])
            store(j, j + 1, 0, QUARTER)

        for j in half_tiles:
            if j == QUARTER_TILES:
                add_x4((j, 0), 0, QUARTER)
                add_x4((j, 0), QUARTER, HALF)
                add_xr((j, 0), QUARTER, HALF, stop=True)
            elif j < EARLY_TILES:
                add_xr((j, 0), QUARTER, HALF)
                add_x4((j, 0), 0, HALF, stop=True)
            else:
                add_x4((j, 0), 0, HALF)
                add_xr((j, 0), 0, HALF, stop=True)
            drain((j, 0), HALF, j == QUARTER_TILES)
            place = j - QUARTER_TILES
            if place < SINGLE_HALVES:
                store(j, j + 1, 0, HALF)
            elif (place - SINGLE_HALVES) % 2 == 1:
                store(j - 1, j + 1, 0, HALF)
            if j == QUARTER_TILES:
                prepare_second_half()

        for j in quarter_tiles:
            add_x4((j, QUARTER), QUARTER, HALF)
            add_xr((j, QUARTER), QUARTER, HALF, stop=True)
            drain((j, QUARTER), QUARTER, False)

        def deal_columns(g):
            nc.scalar.copy(
                out=w4[:, w4_cut + 4 * P * g : w4_cut + 4 * P * (g + 1)].bitcast(U16).rearrange("k (i p) -> k i p", i=2),
                in_=w4_late[:, 4 * P * g : 4 * P * (g + 1)].bitcast(U16).rearrange("k (p i) -> k i p", i=2),
            )

        def deal_bias():
            nc.vector.tensor_copy(
                out=b_pairs[:].rearrange("a (g i c) -> a g i c", i=2, c=QUADRANT),
                in_=b_rows[:, b_cut:].rearrange("a (g c i) -> a g i c", i=2, c=QUADRANT),
            )

        late_halves = range(QUARTER_TILES + SECOND_HALF_GROUP, QUARTER_TILES + HALF_TILES)
        units = [(j, HALF) for j in range(QUARTER_TILES + SECOND_HALF_GROUP)]
        units += [(j, t0) for j in whole_tiles for t0 in (0, HALF)]
        units += [(j, HALF) for j in late_halves]
        last_quarters = (HALF, HALF + QUARTER)
        for t0 in last_quarters:
            add_x4((0, t0), t0, t0 + QUARTER)
        for j in quarter_tiles[1:]:
            add_x4((j, HALF), HALF, T)
        for u, (j, t0) in enumerate(units):
            if u == 0:
                for t1 in last_quarters:
                    add_xr((0, t1), t1, t1 + QUARTER, stop=True)
                    drain((0, t1), QUARTER, t1 == HALF)
            else:
                if j not in quarter_tiles:
                    add_x4((j, t0), t0, t0 + HALF)
                add_xr((j, t0), t0, t0 + HALF, stop=True)
                drain((j, t0), HALF, u % 2 == 0)
            if u == 0:
                deal_bias()
            if u == 2:
                nc.vector.transpose(b_cols[:, b_cut:], b_pairs[:])
            if u in (1, 3):
                deal_columns(u // 2)
            if j in quarter_tiles:
                store(j, j + 1, QUARTER, T)
            elif j in whole_tiles:
                if t0 == HALF and j % 2 == 1:
                    nc.sync.dma_start(
                        out=out[P * (j - 1) : P * (j + 1), :].rearrange("(p i) t -> p (i t)", i=2),
                        in_=result[:, j - 1 : j + 1, :].rearrange("p i t -> p (i t)"),
                    )
            elif j + 1 == late_halves.start:
                store(QUARTER_TILES, j + 1, HALF, T)
            elif j + 1 == late_halves.stop:
                store(late_halves.start, j + 1, HALF, T)
